import numpy as np
import ml_dtypes


def mxq(x, axis, fmt="e4m3"):
    dtype, down = {"e4m3": (ml_dtypes.float8_e4m3fn, 7), "e5m2": (ml_dtypes.float8_e5m2, 14)}[fmt]
    v = np.moveaxis(np.asarray(x, np.float32).astype(ml_dtypes.bfloat16).astype(np.float64), axis, -1)
    blocks = v.reshape(v.shape[:-1] + (-1, 32))
    amax = np.abs(blocks).max(-1, keepdims=True)
    byte = np.maximum(np.where(amax > 0, np.frexp(amax)[1] - 1 + 127, 0) - down, 1)
    scale = np.exp2(byte - 127.0)
    codes = (blocks / scale).astype(np.float32).astype(dtype).astype(np.float64)
    return np.moveaxis((codes * scale).reshape(v.shape), -1, axis)


WIDE = False


def mx_kscale(k):
    if not WIDE:
        return np.ones(k)
    levels = np.array([10, -10, 5, -5, 0])
    if k % 512:
        return np.exp2(np.random.permutation(np.resize(levels, k // 32))).repeat(32)
    a = np.empty((k // 512, 16))
    for p in range(k // 512):
        a[p, :8] = np.random.permutation(np.resize(levels, 8))
        for g in range(8):
            far = levels[np.abs(levels - a[p, g]) >= 10]
            a[p, g + 8] = far[np.random.randint(len(far))]
    return np.exp2(a.ravel()).repeat(32)


def f64(x):
    return np.asarray(x).astype(np.float64)


def striped(idx):
    return np.tile(idx.reshape(-1, 16).T, (8, 1)).astype(np.uint16)


def unstriped(offs):
    return offs[:16].T.reshape(-1).astype(np.int64)


def pack_weight(w):
    k, n = w.shape
    w = f64(np.asarray(w, np.float32).astype(ml_dtypes.bfloat16)).reshape(k // 32, 32, n)
    amax = np.abs(w).max(1)
    byte = np.clip(np.where(amax > 0, np.frexp(amax)[1] - 1 + 127 - 7, 1), 1, 254)
    scaled = (w * np.exp2(127.0 - byte)[:, None, :]).reshape(k, n).astype(np.float32)
    words = np.ascontiguousarray(scaled.reshape(k // 512, 128, 4, n).transpose(0, 1, 3, 2)).astype(ml_dtypes.float8_e4m3fn).view(np.uint8)
    return words, np.ascontiguousarray(byte.astype(np.uint8).reshape(k // 512, 16, n))


def unpack_weight(words, scales):
    g, p, n, _ = words.shape
    vals = np.ascontiguousarray(words).view(ml_dtypes.float8_e4m3fn).astype(np.float64) * np.repeat(np.exp2(scales.astype(np.float64) - 127.0), 8, axis=1)[..., None]
    return vals.transpose(0, 1, 3, 2).reshape(g * 512, n)


def relu(v):
    return np.maximum(v, 0.0)


K, T, S, V, N = 512, 4096, 1024, 512, 256


def setup_inputs():
    n = np.random.standard_normal
    s = mx_kscale(K)[:, None]
    packed_w1 = pack_weight(n((K, N)) / np.sqrt(K) / s)
    packed_w2 = pack_weight(n((K, N)) / np.sqrt(K) / s)
    return {
        "xT": (n((K, T)) * s).astype(np.float32),
        "sT": (n((K, V)) * s).astype(np.float32),
        "w1_words": packed_w1[0],
        "w1_scales": packed_w1[1],
        "w2_words": packed_w2[0],
        "w2_scales": packed_w2[1],
        "offs": striped(np.random.permutation(T)[:S]),
        "par": striped(np.random.randint(0, V, S)),
    }


def reference(xT, sT, w1_words, w1_scales, w2_words, w2_scales, offs, par):
    xq = mxq(f64(xT)[:, unstriped(offs)], 0, "e4m3")
    y = unpack_weight(w1_words, w1_scales).T @ xq
    t = unpack_weight(w2_words, w2_scales).T @ mxq(f64(sT), 0, "e4m3")
    return relu(y + t[:, unstriped(par)])

@@ -1,0 +1,142 @@
+from contextlib import ExitStack
+
+import concourse.mybir as mybir
+
+K, T, S, V, N = 512, 4096, 1024, 512, 256
+FLOPS = 2 * K * N * (S + V)
+
+F32 = mybir.dt.float32
+BF16 = mybir.dt.bfloat16
+I32 = mybir.dt.int32
+U32 = mybir.dt.uint32
+U16 = mybir.dt.uint16
+U8 = mybir.dt.uint8
+FP8X4 = mybir.dt.float8_e4m3fn_x4
+COPY = mybir.ActivationFunctionType.Copy
+RELU = mybir.ActivationFunctionType.Relu
+ADD = mybir.AluOpType.add
+
+P = 128
+PACK = 4
+HALF = S // 2
+LIST_COLS = HALF // 16
+SPARE = 32
+LAST_CHUNKS = (1024, 1024, 1024, 512, 256, 256)
+CAST_ON_VECTOR = (2, 4, 5)
+
+
+def tile_picked_fpn_relu_e_kernel(
+    tc, xT, sT, w1_words, w1_scales, w2_words, w2_scales, offs, par, out
+):
+    nc = tc.nc
+    with ExitStack() as ctx:
+        keep = ctx.enter_context(tc.tile_pool(name="keep", bufs=1))
+        psum = ctx.enter_context(tc.psum_pool(name="psum", bufs=1))
+
+        x_rows = xT.rearrange("(p j) c -> p j c", j=PACK)
+
+        def load_scales(scales, planes):
+            for q in range(4):
+                nc.sync.dma_start(
+                    planes[32 * q + 4 : 32 * q + 8, :N].bitcast(I32),
+                    scales[0, 4 * q : 4 * q + 4, :].bitcast(I32),
+                )
+
+        def load_words(words, name):
+            codes = keep.tile([P, N], I32, name=name, align_bytes=64)
+            nc.sync.dma_start(codes[:], words[0].rearrange("p n t -> p (n t)").bitcast(I32))
+            return codes
+
+        def quantize(grouped, plane, name):
+            codes = keep.tile([P, HALF], U32, name=name + "_codes", align_bytes=64)
+            nc.vector.quantize_mx(
+                out=codes[:].bitcast(FP8X4), scales=plane[:], in_=grouped[:].rearrange("p c j -> p (c j)")
+            )
+            return codes
+
+        def product(w_codes, w_plane, block, codes, plane, name):
+            acc = psum.tile([P, HALF], F32, name=name)
+            cols = slice(block * P, (block + 1) * P)
+            nc.tensor.matmul_mx(
+                out=acc[:],
+                lhsT=w_codes[:, cols].bitcast(FP8X4),
+                lhsT_scale=w_plane[4:, cols],
+                rhs=codes[:].bitcast(FP8X4),
+                rhs_scale=plane[:],
+                start=True,
+                stop=True,
+            )
+            return acc
+
+        s_raw = keep.tile([P, PACK, V], F32)
+        nc.sync.dma_start(s_raw[:], sT.rearrange("(p j) c -> p j c", j=PACK))
+        s_plane = keep.tile([P, V], U8, align_bytes=64)
+        load_scales(w2_scales, s_plane)
+        w2_codes = load_words(w2_words, "w2_codes")
+        par_list = keep.tile([P, S // 16], U16)
+        nc.sync.dma_start(par_list[:], par)
+
+        x_plane = [keep.tile([P, T], F32, name="x_plane%d" % j) for j in range(PACK)]
+        nc.sync.dma_start(x_plane[2][:], x_rows[:, 2, :])
+        offs_list = keep.tile([P, S // 16], U16)
+        nc.sync.dma_start(offs_list[:], offs)
+        nc.sync.dma_start(x_plane[0][:], x_rows[:, 0, :])
+        picked_plane = [keep.tile([P, HALF], U8, name="picked_plane%d" % h, align_bytes=64) for h in range(2)]
+        load_scales(w1_scales, picked_plane[0])
+        nc.sync.dma_start(x_plane[1][:], x_rows[:, 1, :])
+        edges = [sum(LAST_CHUNKS[:c]) for c in range(len(LAST_CHUNKS) + 1)]
+        for c in range(len(LAST_CHUNKS)):
+            nc.sync.dma_start(x_plane[3][:, edges[c] : edges[c + 1]], x_rows[:, 3, edges[c] : edges[c + 1]])
+        w1_codes = load_words(w1_words, "w1_codes")
+
+        halves = [slice(h * LIST_COLS, (h + 1) * LIST_COLS) for h in range(2)]
+
+        s_grouped = keep.tile([P, V, PACK], BF16, align_bytes=64)
+        nc.vector.tensor_copy(
+            s_grouped[:].rearrange("p (c i) j -> p c j i", i=4),
+            s_raw[:].rearrange("p j (c i) -> p c j i", i=4),
+        )
+        s_codes = quantize(s_grouped, s_plane, "s")
+        parents = {}
+        for block in range(N // P):
+            t_window = keep.tile([P, V + SPARE], F32, name="t_window%d" % block)
+            nc.gpsimd.memset(t_window[:, V:], 0.0)
+            acc = product(w2_codes, s_plane, block, s_codes, s_plane, "t_acc%d" % block)
+            nc.scalar.activation(t_window[:, :V], acc[:], COPY)
+            for h in range(2):
+                parents[h, block] = keep.tile([P, HALF], F32, name="parents%d%d" % (h, block))
+                nc.vector.tensor_copy(parents[h, block][:], t_window[:].indirect(par_list[:, halves[h]]))
+
+        picked = [keep.tile([P, HALF, PACK], BF16, name="picked%d" % h, align_bytes=64) for h in range(2)]
+        dense = keep.tile([P, HALF], BF16)
+        nc.vector.tensor_copy(dense[:], x_plane[2][:].indirect(offs_list[:, halves[1]]))
+        nc.scalar.activation(picked[1][:, :, 2], dense[:], COPY)
+        nc.vector.tensor_copy(picked[0][:, :, 2], x_plane[2][:].indirect(offs_list[:, halves[0]]))
+        for j in (0, 1):
+            for h in range(2):
+                nc.vector.tensor_copy(picked[h][:, :, j], x_plane[j][:].indirect(offs_list[:, halves[h]]))
+
+        x3_rounded = keep.tile([P, T], BF16)
+        for c in range(len(LAST_CHUNKS)):
+            cols = slice(edges[c], edges[c + 1])
+            if c in CAST_ON_VECTOR:
+                nc.vector.tensor_copy(x3_rounded[:, cols], x_plane[3][:, cols])
+            else:
+                nc.scalar.activation(x3_rounded[:, cols], x_plane[3][:, cols], COPY)
+        nc.vector.tensor_copy(picked[0][:, :, 3], x_plane[3][:].indirect(offs_list[:, halves[0]]))
+        nc.scalar.activation(picked[1][:, :, 3], x3_rounded[:].indirect(offs_list[:, halves[1]]), COPY)
+
+        accs = {}
+        for h in range(2):
+            codes = quantize(picked[h], picked_plane[h], "x%d" % h)
+            for block in range(N // P):
+                accs[h, block] = product(
+                    w1_codes, picked_plane[0], block, codes, picked_plane[h], "y_acc%d%d" % (h, block)
+                )
+        for h in range(2):
+            for block in range(N // P):
+                total = keep.tile([P, HALF], F32, name="total%d%d" % (h, block))
+                nc.vector.tensor_tensor(total[:], accs[h, block][:], parents[h, block][:], ADD)
+                result = keep.tile([P, HALF], F32, name="result%d%d" % (h, block))
+                nc.scalar.activation(result[:], total[:], RELU)
+                nc.sync.dma_start(out[block * P : (block + 1) * P, h * HALF : (h + 1) * HALF], result[:])

@@ -18,11 +18,13 @@ ADD = mybir.AluOpType.add
 
 P = 128
 PACK = 4
+BLOCKS = N // P
 HALF = S // 2
-LIST_COLS = HALF // 16
+PIECE = 256
 SPARE = 32
-LAST_CHUNKS = (1024, 1024, 1024, 512, 256, 256)
-CAST_ON_VECTOR = (2, 4, 5)
+S_ON_VECTOR = 352
+LAST_CHUNKS = (1024, 1024, 1024, 512, 384, 128)
+CAST_ON_VECTOR = (1, 2, 4)
 
 
 def tile_picked_fpn_relu_e_kernel(
@@ -47,74 +49,81 @@ def tile_picked_fpn_relu_e_kernel(
             nc.sync.dma_start(codes[:], words[0].rearrange("p n t -> p (n t)").bitcast(I32))
             return codes
 
-        def quantize(grouped, plane, name):
-            codes = keep.tile([P, HALF], U32, name=name + "_codes", align_bytes=64)
+        def quantize(grouped, planes, name):
+            codes = keep.tile([P, grouped.shape[1]], U32, name=name, align_bytes=64)
             nc.vector.quantize_mx(
-                out=codes[:].bitcast(FP8X4), scales=plane[:], in_=grouped[:].rearrange("p c j -> p (c j)")
+                out=codes[:].bitcast(FP8X4), scales=planes[:], in_=grouped.rearrange("p c j -> p (c j)")
             )
             return codes
 
-        def product(w_codes, w_plane, block, codes, plane, name):
-            acc = psum.tile([P, HALF], F32, name=name)
+        def product(w_codes, w_planes, block, codes, planes, bank):
+            acc = psum.tile([P, codes.shape[1]], F32, name="acc", tag="bank%d" % bank)
             cols = slice(block * P, (block + 1) * P)
             nc.tensor.matmul_mx(
                 out=acc[:],
                 lhsT=w_codes[:, cols].bitcast(FP8X4),
-                lhsT_scale=w_plane[4:, cols],
+                lhsT_scale=w_planes[4:, cols],
                 rhs=codes[:].bitcast(FP8X4),
-                rhs_scale=plane[:],
+                rhs_scale=planes[:],
                 start=True,
                 stop=True,
             )
             return acc
 
+        def side_by_side(grouped, rows):
+            return (
+                grouped.rearrange("p (c i) j -> p c j i", i=4),
+                rows.rearrange("p j (c i) -> p c j i", i=4),
+            )
+
         s_raw = keep.tile([P, PACK, V], F32)
         nc.sync.dma_start(s_raw[:], sT.rearrange("(p j) c -> p j c", j=PACK))
-        s_plane = keep.tile([P, V], U8, align_bytes=64)
-        load_scales(w2_scales, s_plane)
+        s_planes = keep.tile([P, V], U8, align_bytes=64)
+        load_scales(w2_scales, s_planes)
         w2_codes = load_words(w2_words, "w2_codes")
         par_list = keep.tile([P, S // 16], U16)
         nc.sync.dma_start(par_list[:], par)
 
         x_plane = [keep.tile([P, T], F32, name="x_plane%d" % j) for j in range(PACK)]
-        nc.sync.dma_start(x_plane[2][:], x_rows[:, 2, :])
+        nc.sync.dma_start(x_plane[0][:], x_rows[:, 0, :])
         offs_list = keep.tile([P, S // 16], U16)
         nc.sync.dma_start(offs_list[:], offs)
-        nc.sync.dma_start(x_plane[0][:], x_rows[:, 0, :])
-        picked_plane = [keep.tile([P, HALF], U8, name="picked_plane%d" % h, align_bytes=64) for h in range(2)]
-        load_scales(w1_scales, picked_plane[0])
         nc.sync.dma_start(x_plane[1][:], x_rows[:, 1, :])
+        piece_planes = [
+            keep.tile([P, PIECE], U8, name="piece_planes%d" % n, align_bytes=64) for n in range(S // PIECE)
+        ]
+        load_scales(w1_scales, piece_planes[0])
+        nc.sync.dma_start(x_plane[2][:], x_rows[:, 2, :])
         edges = [sum(LAST_CHUNKS[:c]) for c in range(len(LAST_CHUNKS) + 1)]
         for c in range(len(LAST_CHUNKS)):
             nc.sync.dma_start(x_plane[3][:, edges[c] : edges[c + 1]], x_rows[:, 3, edges[c] : edges[c + 1]])
         w1_codes = load_words(w1_words, "w1_codes")
 
-        halves = [slice(h * LIST_COLS, (h + 1) * LIST_COLS) for h in range(2)]
+        halves = [slice(h * HALF // 16, (h + 1) * HALF // 16) for h in range(2)]
 
         s_grouped = keep.tile([P, V, PACK], BF16, align_bytes=64)
-        nc.vector.tensor_copy(
-            s_grouped[:].rearrange("p (c i) j -> p c j i", i=4),
-            s_raw[:].rearrange("p j (c i) -> p c j i", i=4),
-        )
-        s_codes = quantize(s_grouped, s_plane, "s")
+        nc.vector.tensor_copy(*side_by_side(s_grouped[:, :S_ON_VECTOR, :], s_raw[:, :, :S_ON_VECTOR]))
+        nc.scalar.copy(*side_by_side(s_grouped[:, S_ON_VECTOR:, :], s_raw[:, :, S_ON_VECTOR:]))
+        s_codes = quantize(s_grouped[:], s_planes, "s_codes")
         parents = {}
-        for block in range(N // P):
+        for block in range(BLOCKS):
             t_window = keep.tile([P, V + SPARE], F32, name="t_window%d" % block)
             nc.gpsimd.memset(t_window[:, V:], 0.0)
-            acc = product(w2_codes, s_plane, block, s_codes, s_plane, "t_acc%d" % block)
-            nc.scalar.activation(t_window[:, :V], acc[:], COPY)
+            acc = product(w2_codes, s_planes, block, s_codes, s_planes, block)
+            nc.scalar.copy(t_window[:, :V], acc[:])
             for h in range(2):
                 parents[h, block] = keep.tile([P, HALF], F32, name="parents%d%d" % (h, block))
                 nc.vector.tensor_copy(parents[h, block][:], t_window[:].indirect(par_list[:, halves[h]]))
 
         picked = [keep.tile([P, HALF, PACK], BF16, name="picked%d" % h, align_bytes=64) for h in range(2)]
-        dense = keep.tile([P, HALF], BF16)
-        nc.vector.tensor_copy(dense[:], x_plane[2][:].indirect(offs_list[:, halves[1]]))
-        nc.scalar.activation(picked[1][:, :, 2], dense[:], COPY)
-        nc.vector.tensor_copy(picked[0][:, :, 2], x_plane[2][:].indirect(offs_list[:, halves[0]]))
-        for j in (0, 1):
+        dense = [keep.tile([P, 2 + h, HALF], BF16, name="dense%d" % h) for h in range(2)]
+        for j in range(2):
             for h in range(2):
-                nc.vector.tensor_copy(picked[h][:, :, j], x_plane[j][:].indirect(offs_list[:, halves[h]]))
+                nc.vector.tensor_copy(dense[h][:, j, :], x_plane[j][:].indirect(offs_list[:, halves[h]]))
+        nc.scalar.copy(*side_by_side(picked[0][:, :, :2], dense[0][:]))
+        nc.vector.tensor_copy(dense[1][:, 2, :], x_plane[2][:].indirect(offs_list[:, halves[1]]))
+        nc.vector.tensor_copy(picked[0][:, :, 2], x_plane[2][:].indirect(offs_list[:, halves[0]]))
+        nc.scalar.copy(*side_by_side(picked[1][:, :, :3], dense[1][:]))
 
         x3_rounded = keep.tile([P, T], BF16)
         for c in range(len(LAST_CHUNKS)):
@@ -127,16 +136,27 @@ def tile_picked_fpn_relu_e_kernel(
         nc.scalar.activation(picked[1][:, :, 3], x3_rounded[:].indirect(offs_list[:, halves[1]]), COPY)
 
         accs = {}
-        for h in range(2):
-            codes = quantize(picked[h], picked_plane[h], "x%d" % h)
-            for block in range(N // P):
-                accs[h, block] = product(
-                    w1_codes, picked_plane[0], block, codes, picked_plane[h], "y_acc%d%d" % (h, block)
+
+        def multiply(n):
+            h, first = divmod(n * PIECE, HALF)
+            codes = quantize(picked[h][:, first : first + PIECE, :], piece_planes[n], "piece_codes%d" % n)
+            for block in range(BLOCKS):
+                bank = (BLOCKS * (n + 1) + block) % 8
+                accs[n, block] = product(w1_codes, piece_planes[0], block, codes, piece_planes[n], bank)
+
+        def finish(n):
+            h, first = divmod(n * PIECE, HALF)
+            for block in range(BLOCKS):
+                total = keep.tile([P, PIECE], F32, name="total%d%d" % (n, block))
+                nc.vector.tensor_tensor(
+                    total[:], accs[n, block][:], parents[h, block][:, first : first + PIECE], ADD
                 )
-        for h in range(2):
-            for block in range(N // P):
-                total = keep.tile([P, HALF], F32, name="total%d%d" % (h, block))
-                nc.vector.tensor_tensor(total[:], accs[h, block][:], parents[h, block][:], ADD)
-                result = keep.tile([P, HALF], F32, name="result%d%d" % (h, block))
+                result = keep.tile([P, PIECE], F32, name="result%d%d" % (n, block))
                 nc.scalar.activation(result[:], total[:], RELU)
-                nc.sync.dma_start(out[block * P : (block + 1) * P, h * HALF : (h + 1) * HALF], result[:])
+                nc.sync.dma_start(out[block * P : (block + 1) * P, n * PIECE : (n + 1) * PIECE], result[:])
+
+        multiply(0)
+        for n in range(1, S // PIECE):
+            multiply(n)
+            finish(n - 1)
+        finish(S // PIECE - 1)

@@ -56,11 +56,10 @@ def tile_picked_fpn_relu_e_kernel(
             )
             return codes
 
-        def product(w_codes, w_planes, block, codes, planes, bank):
-            acc = psum.tile([P, codes.shape[1]], F32, name="acc", tag="bank%d" % bank)
+        def product(acc, w_codes, w_planes, block, codes, planes):
             cols = slice(block * P, (block + 1) * P)
             nc.tensor.matmul_mx(
-                out=acc[:],
+                out=acc,
                 lhsT=w_codes[:, cols].bitcast(FP8X4),
                 lhsT_scale=w_planes[4:, cols],
                 rhs=codes[:].bitcast(FP8X4),
@@ -68,7 +67,6 @@ def tile_picked_fpn_relu_e_kernel(
                 start=True,
                 stop=True,
             )
-            return acc
 
         def side_by_side(grouped, rows):
             return (
@@ -90,7 +88,8 @@ def tile_picked_fpn_relu_e_kernel(
         nc.sync.dma_start(offs_list[:], offs)
         nc.sync.dma_start(x_plane[1][:], x_rows[:, 1, :])
         piece_planes = [
-            keep.tile([P, PIECE], U8, name="piece_planes%d" % n, align_bytes=64) for n in range(S // PIECE)
+            keep.tile([P, width], U8, name="piece_planes%d" % n, align_bytes=64)
+            for n, width in enumerate((PIECE, PIECE, HALF))
         ]
         load_scales(w1_scales, piece_planes[0])
         nc.sync.dma_start(x_plane[2][:], x_rows[:, 2, :])
@@ -105,15 +104,15 @@ def tile_picked_fpn_relu_e_kernel(
         nc.vector.tensor_copy(*side_by_side(s_grouped[:, :S_ON_VECTOR, :], s_raw[:, :, :S_ON_VECTOR]))
         nc.scalar.copy(*side_by_side(s_grouped[:, S_ON_VECTOR:, :], s_raw[:, :, S_ON_VECTOR:]))
         s_codes = quantize(s_grouped[:], s_planes, "s_codes")
-        parents = {}
+        parents = [keep.tile([P, BLOCKS, HALF], F32, name="parents%d" % h) for h in range(2)]
         for block in range(BLOCKS):
             t_window = keep.tile([P, V + SPARE], F32, name="t_window%d" % block)
             nc.gpsimd.memset(t_window[:, V:], 0.0)
-            acc = product(w2_codes, s_planes, block, s_codes, s_planes, block)
+            acc = psum.tile([P, V], F32, name="t_acc%d" % block)
+            product(acc[:], w2_codes, s_planes, block, s_codes, s_planes)
             nc.scalar.copy(t_window[:, :V], acc[:])
             for h in range(2):
-                parents[h, block] = keep.tile([P, HALF], F32, name="parents%d%d" % (h, block))
-                nc.vector.tensor_copy(parents[h, block][:], t_window[:].indirect(par_list[:, halves[h]]))
+                nc.vector.tensor_copy(parents[h][:, block, :], t_window[:].indirect(par_list[:, halves[h]]))
 
         picked = [keep.tile([P, HALF, PACK], BF16, name="picked%d" % h, align_bytes=64) for h in range(2)]
         dense = [keep.tile([P, 2 + h, HALF], BF16, name="dense%d" % h) for h in range(2)]
@@ -121,9 +120,12 @@ def tile_picked_fpn_relu_e_kernel(
             for h in range(2):
                 nc.vector.tensor_copy(dense[h][:, j, :], x_plane[j][:].indirect(offs_list[:, halves[h]]))
         nc.scalar.copy(*side_by_side(picked[0][:, :, :2], dense[0][:]))
-        nc.vector.tensor_copy(dense[1][:, 2, :], x_plane[2][:].indirect(offs_list[:, halves[1]]))
+        for first in range(0, HALF, PIECE):
+            cols = slice(first, first + PIECE)
+            entries = slice((HALF + first) // 16, (HALF + first + PIECE) // 16)
+            nc.vector.tensor_copy(dense[1][:, 2, cols], x_plane[2][:].indirect(offs_list[:, entries]))
+            nc.scalar.copy(*side_by_side(picked[1][:, cols, :3], dense[1][:, :, cols]))
         nc.vector.tensor_copy(picked[0][:, :, 2], x_plane[2][:].indirect(offs_list[:, halves[0]]))
-        nc.scalar.copy(*side_by_side(picked[1][:, :, :3], dense[1][:]))
 
         x3_rounded = keep.tile([P, T], BF16)
         for c in range(len(LAST_CHUNKS)):
@@ -135,28 +137,38 @@ def tile_picked_fpn_relu_e_kernel(
         nc.vector.tensor_copy(picked[0][:, :, 3], x_plane[3][:].indirect(offs_list[:, halves[0]]))
         nc.scalar.activation(picked[1][:, :, 3], x3_rounded[:].indirect(offs_list[:, halves[1]]), COPY)
 
-        accs = {}
+        def add_parents(acc, h, block, n):
+            name = "%d%d%d" % (h, block, n)
+            cols = slice(n * PIECE, (n + 1) * PIECE)
+            total = keep.tile([P, PIECE], F32, name="total" + name)
+            nc.vector.tensor_tensor(total[:], acc, parents[h][:, block, cols], ADD)
+            return total, h, block, n
 
-        def multiply(n):
-            h, first = divmod(n * PIECE, HALF)
-            codes = quantize(picked[h][:, first : first + PIECE, :], piece_planes[n], "piece_codes%d" % n)
-            for block in range(BLOCKS):
-                bank = (BLOCKS * (n + 1) + block) % 8
-                accs[n, block] = product(w1_codes, piece_planes[0], block, codes, piece_planes[n], bank)
-
-        def finish(n):
-            h, first = divmod(n * PIECE, HALF)
-            for block in range(BLOCKS):
-                total = keep.tile([P, PIECE], F32, name="total%d%d" % (n, block))
-                nc.vector.tensor_tensor(
-                    total[:], accs[n, block][:], parents[h, block][:, first : first + PIECE], ADD
-                )
-                result = keep.tile([P, PIECE], F32, name="result%d%d" % (n, block))
+        def finish(total, h, block, n, on_vector=False):
+            result = keep.tile([P, PIECE], F32, name="result%d%d%d" % (h, block, n))
+            if on_vector:
+                nc.vector.tensor_scalar_max(result[:], total[:], 0.0)
+            else:
                 nc.scalar.activation(result[:], total[:], RELU)
-                nc.sync.dma_start(out[block * P : (block + 1) * P, n * PIECE : (n + 1) * PIECE], result[:])
+            first = h * HALF + n * PIECE
+            nc.sync.dma_start(out[block * P : (block + 1) * P, first : first + PIECE], result[:])
 
-        multiply(0)
-        for n in range(1, S // PIECE):
-            multiply(n)
-            finish(n - 1)
-        finish(S // PIECE - 1)
+        sums = []
+        for n in range(HALF // PIECE):
+            codes = quantize(picked[0][:, n * PIECE : (n + 1) * PIECE, :], piece_planes[n], "piece_codes%d" % n)
+            for block in range(BLOCKS):
+                acc = psum.tile([P, PIECE], F32, name="first_acc%d%d" % (n, block))
+                product(acc[:], w1_codes, piece_planes[0], block, codes, piece_planes[n])
+                sums.append((acc[:], 0, block, n))
+        codes = quantize(picked[1][:], piece_planes[2], "second_codes")
+        for block in range(BLOCKS):
+            acc = psum.tile([P, HALF], F32, name="second_acc%d" % block)
+            product(acc[:], w1_codes, piece_planes[0], block, codes, piece_planes[2])
+            for n in range(HALF // PIECE):
+                sums.append((acc[:, n * PIECE : (n + 1) * PIECE], 1, block, n))
+
+        for piece in sums[:-2]:
+            finish(*add_parents(*piece))
+        last = [add_parents(*piece) for piece in sums[-2:]]
+        finish(*last[0], on_vector=True)
+        finish(*last[1])

@@ -22,9 +22,10 @@ BLOCKS = N // P
 HALF = S // 2
 PIECE = 256
 SPARE = 32
+W2_ROW = 4
 S_ON_VECTOR = 352
-LAST_CHUNKS = (1024, 1024, 1024, 512, 384, 128)
-CAST_ON_VECTOR = (1, 2, 4)
+LAST_CHUNKS = (2048, 1408, 512, 128)
+ROUNDED_ON_VECTOR = (1024, 896, 384, 0)
 
 
 def tile_picked_fpn_relu_e_kernel(
@@ -37,10 +38,10 @@ def tile_picked_fpn_relu_e_kernel(
 
         x_rows = xT.rearrange("(p j) c -> p j c", j=PACK)
 
-        def load_scales(scales, planes):
+        def load_scales(scales, planes, row):
             for q in range(4):
                 nc.sync.dma_start(
-                    planes[32 * q + 4 : 32 * q + 8, :N].bitcast(I32),
+                    planes[32 * q + row : 32 * q + row + 4, :N].bitcast(I32),
                     scales[0, 4 * q : 4 * q + 4, :].bitcast(I32),
                 )
 
@@ -61,7 +62,7 @@ def tile_picked_fpn_relu_e_kernel(
             nc.tensor.matmul_mx(
                 out=acc,
                 lhsT=w_codes[:, cols].bitcast(FP8X4),
-                lhsT_scale=w_planes[4:, cols],
+                lhsT_scale=w_planes[:, cols],
                 rhs=codes[:].bitcast(FP8X4),
                 rhs_scale=planes[:],
                 start=True,
@@ -77,7 +78,7 @@ def tile_picked_fpn_relu_e_kernel(
         s_raw = keep.tile([P, PACK, V], F32)
         nc.sync.dma_start(s_raw[:], sT.rearrange("(p j) c -> p j c", j=PACK))
         s_planes = keep.tile([P, V], U8, align_bytes=64)
-        load_scales(w2_scales, s_planes)
+        load_scales(w2_scales, s_planes, W2_ROW)
         w2_codes = load_words(w2_words, "w2_codes")
         par_list = keep.tile([P, S // 16], U16)
         nc.sync.dma_start(par_list[:], par)
@@ -91,12 +92,14 @@ def tile_picked_fpn_relu_e_kernel(
             keep.tile([P, width], U8, name="piece_planes%d" % n, align_bytes=64)
             for n, width in enumerate((PIECE, PIECE, HALF))
         ]
-        load_scales(w1_scales, piece_planes[0])
         nc.sync.dma_start(x_plane[2][:], x_rows[:, 2, :])
         edges = [sum(LAST_CHUNKS[:c]) for c in range(len(LAST_CHUNKS) + 1)]
         for c in range(len(LAST_CHUNKS)):
             nc.sync.dma_start(x_plane[3][:, edges[c] : edges[c + 1]], x_rows[:, 3, edges[c] : edges[c + 1]])
         w1_codes = load_words(w1_words, "w1_codes")
+        w1_planes = keep.tile([P, N], U8, align_bytes=64)
+        nc.gpsimd.memset(w1_planes[:], 0)
+        load_scales(w1_scales, w1_planes, 0)
 
         halves = [slice(h * HALF // 16, (h + 1) * HALF // 16) for h in range(2)]
 
@@ -109,7 +112,7 @@ def tile_picked_fpn_relu_e_kernel(
             t_window = keep.tile([P, V + SPARE], F32, name="t_window%d" % block)
             nc.gpsimd.memset(t_window[:, V:], 0.0)
             acc = psum.tile([P, V], F32, name="t_acc%d" % block)
-            product(acc[:], w2_codes, s_planes, block, s_codes, s_planes)
+            product(acc[:], w2_codes, s_planes[W2_ROW:], block, s_codes, s_planes)
             nc.scalar.copy(t_window[:, :V], acc[:])
             for h in range(2):
                 nc.vector.tensor_copy(parents[h][:, block, :], t_window[:].indirect(par_list[:, halves[h]]))
@@ -129,46 +132,49 @@ def tile_picked_fpn_relu_e_kernel(
 
         x3_rounded = keep.tile([P, T], BF16)
         for c in range(len(LAST_CHUNKS)):
-            cols = slice(edges[c], edges[c + 1])
-            if c in CAST_ON_VECTOR:
-                nc.vector.tensor_copy(x3_rounded[:, cols], x_plane[3][:, cols])
-            else:
-                nc.scalar.activation(x3_rounded[:, cols], x_plane[3][:, cols], COPY)
+            cut = edges[c] + ROUNDED_ON_VECTOR[c]
+            if cut > edges[c]:
+                nc.vector.tensor_copy(x3_rounded[:, edges[c] : cut], x_plane[3][:, edges[c] : cut])
+            nc.scalar.activation(x3_rounded[:, cut : edges[c + 1]], x_plane[3][:, cut : edges[c + 1]], COPY)
         nc.vector.tensor_copy(picked[0][:, :, 3], x_plane[3][:].indirect(offs_list[:, halves[0]]))
         nc.scalar.activation(picked[1][:, :, 3], x3_rounded[:].indirect(offs_list[:, halves[1]]), COPY)
 
-        def add_parents(acc, h, block, n):
-            name = "%d%d%d" % (h, block, n)
-            cols = slice(n * PIECE, (n + 1) * PIECE)
-            total = keep.tile([P, PIECE], F32, name="total" + name)
-            nc.vector.tensor_tensor(total[:], acc, parents[h][:, block, cols], ADD)
-            return total, h, block, n
-
-        def finish(total, h, block, n, on_vector=False):
-            result = keep.tile([P, PIECE], F32, name="result%d%d%d" % (h, block, n))
-            if on_vector:
-                nc.vector.tensor_scalar_max(result[:], total[:], 0.0)
-            else:
-                nc.scalar.activation(result[:], total[:], RELU)
-            first = h * HALF + n * PIECE
-            nc.sync.dma_start(out[block * P : (block + 1) * P, first : first + PIECE], result[:])
-
-        sums = []
+        accs = {}
         for n in range(HALF // PIECE):
-            codes = quantize(picked[0][:, n * PIECE : (n + 1) * PIECE, :], piece_planes[n], "piece_codes%d" % n)
+            cols = slice(n * PIECE, (n + 1) * PIECE)
+            codes = quantize(picked[0][:, cols, :], piece_planes[n], "piece_codes%d" % n)
             for block in range(BLOCKS):
                 acc = psum.tile([P, PIECE], F32, name="first_acc%d%d" % (n, block))
-                product(acc[:], w1_codes, piece_planes[0], block, codes, piece_planes[n])
-                sums.append((acc[:], 0, block, n))
+                product(acc[:], w1_codes, w1_planes, block, codes, piece_planes[n])
+                accs[0, block, n] = acc[:]
         codes = quantize(picked[1][:], piece_planes[2], "second_codes")
         for block in range(BLOCKS):
             acc = psum.tile([P, HALF], F32, name="second_acc%d" % block)
-            product(acc[:], w1_codes, piece_planes[0], block, codes, piece_planes[2])
+            product(acc[:], w1_codes, w1_planes, block, codes, piece_planes[2])
             for n in range(HALF // PIECE):
-                sums.append((acc[:, n * PIECE : (n + 1) * PIECE], 1, block, n))
+                accs[1, block, n] = acc[:, n * PIECE : (n + 1) * PIECE]
 
-        for piece in sums[:-2]:
-            finish(*add_parents(*piece))
-        last = [add_parents(*piece) for piece in sums[-2:]]
-        finish(*last[0], on_vector=True)
-        finish(*last[1])
+        def add_parents(h, block, n, total):
+            nc.vector.tensor_tensor(
+                total, accs[h, block, n], parents[h][:, block, n * PIECE : (n + 1) * PIECE], ADD
+            )
+
+        for n in range(HALF // PIECE):
+            for block in range(BLOCKS):
+                total = keep.tile([P, PIECE], F32, name="total%d%d" % (n, block))
+                add_parents(0, block, n, total[:])
+                result = keep.tile([P, PIECE], F32, name="result%d%d" % (n, block))
+                nc.scalar.activation(result[:], total[:], RELU)
+                nc.sync.dma_start(out[block * P : (block + 1) * P, n * PIECE : (n + 1) * PIECE], result[:])
+        for block in range(BLOCKS):
+            total = keep.tile([P, HALF], F32, name="second_total%d" % block)
+            result = keep.tile([P, HALF], F32, name="second_result%d" % block)
+            pieces = [slice(n * PIECE, (n + 1) * PIECE) for n in range(HALF // PIECE)]
+            for n, cols in enumerate(pieces):
+                add_parents(1, block, n, total[:, cols])
+            for cols in pieces:
+                if block == BLOCKS - 1:
+                    nc.vector.tensor_scalar_max(result[:, cols], total[:, cols], 0.0)
+                else:
+                    nc.scalar.activation(result[:, cols], total[:, cols], RELU)
+            nc.sync.dma_start(out[block * P : (block + 1) * P, HALF:], result[:])

@@ -63,8 +63,8 @@ def tile_picked_fpn_relu_e_kernel(
                 out=acc,
                 lhsT=w_codes[:, cols].bitcast(FP8X4),
                 lhsT_scale=w_planes[:, cols],
-                rhs=codes[:].bitcast(FP8X4),
-                rhs_scale=planes[:],
+                rhs=codes.bitcast(FP8X4),
+                rhs_scale=planes,
                 start=True,
                 stop=True,
             )
@@ -104,30 +104,41 @@ def tile_picked_fpn_relu_e_kernel(
         halves = [slice(h * HALF // 16, (h + 1) * HALF // 16) for h in range(2)]
 
         s_grouped = keep.tile([P, V, PACK], BF16, align_bytes=64)
-        nc.vector.tensor_copy(*side_by_side(s_grouped[:, :S_ON_VECTOR, :], s_raw[:, :, :S_ON_VECTOR]))
+        for cols in (slice(0, PIECE), slice(PIECE, S_ON_VECTOR)):
+            nc.vector.tensor_copy(*side_by_side(s_grouped[:, cols, :], s_raw[:, :, cols]))
         nc.scalar.copy(*side_by_side(s_grouped[:, S_ON_VECTOR:, :], s_raw[:, :, S_ON_VECTOR:]))
-        s_codes = quantize(s_grouped[:], s_planes, "s_codes")
+        s_codes = keep.tile([P, V], U32, align_bytes=64)
+        s_cols = [slice(0, PIECE), slice(PIECE, V)]
+        for cols in s_cols:
+            nc.vector.quantize_mx(
+                out=s_codes[:, cols].bitcast(FP8X4),
+                scales=s_planes[:, cols],
+                in_=s_grouped[:, cols, :].rearrange("p c j -> p (c j)"),
+            )
         parents = [keep.tile([P, BLOCKS, HALF], F32, name="parents%d" % h) for h in range(2)]
         for block in range(BLOCKS):
             t_window = keep.tile([P, V + SPARE], F32, name="t_window%d" % block)
             nc.gpsimd.memset(t_window[:, V:], 0.0)
-            acc = psum.tile([P, V], F32, name="t_acc%d" % block)
-            product(acc[:], w2_codes, s_planes[W2_ROW:], block, s_codes, s_planes)
-            nc.scalar.copy(t_window[:, :V], acc[:])
+            for n, cols in enumerate(s_cols):
+                acc = psum.tile([P, HALF], F32, name="t_acc%d%d" % (block, n), tag="bank%d" % (2 * block + n))
+                product(acc[:, :PIECE], w2_codes, s_planes[W2_ROW:], block, s_codes[:, cols], s_planes[:, cols])
+                if block == 0 and n == 1:
+                    nc.vector.tensor_copy(t_window[:, cols], acc[:, :PIECE])
+                else:
+                    nc.scalar.copy(t_window[:, cols], acc[:, :PIECE])
             for h in range(2):
                 nc.vector.tensor_copy(parents[h][:, block, :], t_window[:].indirect(par_list[:, halves[h]]))
 
         picked = [keep.tile([P, HALF, PACK], BF16, name="picked%d" % h, align_bytes=64) for h in range(2)]
-        dense = [keep.tile([P, 2 + h, HALF], BF16, name="dense%d" % h) for h in range(2)]
+        dense = keep.tile([P, 3, S], BF16, name="dense")
         for j in range(2):
-            for h in range(2):
-                nc.vector.tensor_copy(dense[h][:, j, :], x_plane[j][:].indirect(offs_list[:, halves[h]]))
-        nc.scalar.copy(*side_by_side(picked[0][:, :, :2], dense[0][:]))
+            nc.vector.tensor_copy(dense[:, j, :], x_plane[j][:].indirect(offs_list[:]))
+        nc.scalar.copy(*side_by_side(picked[0][:, :, :2], dense[:, :2, :HALF]))
         for first in range(0, HALF, PIECE):
-            cols = slice(first, first + PIECE)
-            entries = slice((HALF + first) // 16, (HALF + first + PIECE) // 16)
-            nc.vector.tensor_copy(dense[1][:, 2, cols], x_plane[2][:].indirect(offs_list[:, entries]))
-            nc.scalar.copy(*side_by_side(picked[1][:, cols, :3], dense[1][:, :, cols]))
+            cols = slice(HALF + first, HALF + first + PIECE)
+            entries = slice(cols.start // 16, cols.stop // 16)
+            nc.vector.tensor_copy(dense[:, 2, cols], x_plane[2][:].indirect(offs_list[:, entries]))
+            nc.scalar.copy(*side_by_side(picked[1][:, first : first + PIECE, :3], dense[:, :, cols]))
         nc.vector.tensor_copy(picked[0][:, :, 2], x_plane[2][:].indirect(offs_list[:, halves[0]]))
 
         x3_rounded = keep.tile([P, T], BF16)
@@ -145,12 +156,12 @@ def tile_picked_fpn_relu_e_kernel(
             codes = quantize(picked[0][:, cols, :], piece_planes[n], "piece_codes%d" % n)
             for block in range(BLOCKS):
                 acc = psum.tile([P, PIECE], F32, name="first_acc%d%d" % (n, block))
-                product(acc[:], w1_codes, w1_planes, block, codes, piece_planes[n])
+                product(acc[:], w1_codes, w1_planes, block, codes[:], piece_planes[n][:])
                 accs[0, block, n] = acc[:]
         codes = quantize(picked[1][:], piece_planes[2], "second_codes")
         for block in range(BLOCKS):
-            acc = psum.tile([P, HALF], F32, name="second_acc%d" % block)
-            product(acc[:], w1_codes, w1_planes, block, codes, piece_planes[2])
+            acc = psum.tile([P, HALF], F32, name="second_acc%d" % block, tag="bank%d" % block)
+            product(acc[:], w1_codes, w1_planes, block, codes[:], piece_planes[2][:])
             for n in range(HALF // PIECE):
                 accs[1, block, n] = acc[:, n * PIECE : (n + 1) * PIECE]
 

@@ -24,8 +24,8 @@ PIECE = 256
 SPARE = 32
 W2_ROW = 4
 S_ON_VECTOR = 352
-LAST_CHUNKS = (2048, 1408, 512, 128)
-ROUNDED_ON_VECTOR = (1024, 896, 384, 0)
+LAST_CHUNKS = (2752, 1024, 320)
+ROUNDED_ON_VECTOR = (1792, 576, 0)
 
 
 def tile_picked_fpn_relu_e_kernel(

@@ -24,8 +24,8 @@ PIECE = 256
 SPARE = 32
 W2_ROW = 4
 S_ON_VECTOR = 352
-LAST_CHUNKS = (2752, 1024, 320)
-ROUNDED_ON_VECTOR = (1792, 576, 0)
+LAST_CHUNKS = (2816, 1024, 256)
+ROUNDED_ON_VECTOR = (1856, 640, 0)
 
 
 def tile_picked_fpn_relu_e_kernel(
@@ -160,10 +160,11 @@ def tile_picked_fpn_relu_e_kernel(
                 accs[0, block, n] = acc[:]
         codes = quantize(picked[1][:], piece_planes[2], "second_codes")
         for block in range(BLOCKS):
-            acc = psum.tile([P, HALF], F32, name="second_acc%d" % block, tag="bank%d" % block)
-            product(acc[:], w1_codes, w1_planes, block, codes[:], piece_planes[2][:])
             for n in range(HALF // PIECE):
-                accs[1, block, n] = acc[:, n * PIECE : (n + 1) * PIECE]
+                cols = slice(n * PIECE, (n + 1) * PIECE)
+                acc = psum.tile([P, HALF], F32, name="second_acc%d%d" % (block, n), tag="bank%d" % (2 * block + n))
+                product(acc[:, :PIECE], w1_codes, w1_planes, block, codes[:, cols], piece_planes[2][:, cols])
+                accs[1, block, n] = acc[:, :PIECE]
 
         def add_parents(h, block, n, total):
             nc.vector.tensor_tensor(
@@ -182,10 +183,15 @@ def tile_picked_fpn_relu_e_kernel(
             result = keep.tile([P, HALF], F32, name="second_result%d" % block)
             pieces = [slice(n * PIECE, (n + 1) * PIECE) for n in range(HALF // PIECE)]
             for n, cols in enumerate(pieces):
-                add_parents(1, block, n, total[:, cols])
-            for cols in pieces:
-                if block == BLOCKS - 1:
-                    nc.vector.tensor_scalar_max(result[:, cols], total[:, cols], 0.0)
-                else:
+                if (block, n) != (BLOCKS - 1, 1):
+                    add_parents(1, block, n, total[:, cols])
                     nc.scalar.activation(result[:, cols], total[:, cols], RELU)
+                    continue
+                ends = [slice(PIECE + g * P, PIECE + (g + 1) * P) for g in range(2)]
+                for g, part in enumerate(ends):
+                    nc.vector.tensor_tensor(
+                        total[:, part], accs[1, block, n][:, g * P : (g + 1) * P], parents[1][:, block, part], ADD
+                    )
+                for part in ends:
+                    nc.vector.tensor_scalar_max(result[:, part], total[:, part], 0.0)
             nc.sync.dma_start(out[block * P : (block + 1) * P, HALF:], result[:])

@@ -24,8 +24,7 @@ PIECE = 256
 SPARE = 32
 W2_ROW = 4
 S_ON_VECTOR = 352
-LAST_CHUNKS = (2816, 1024, 256)
-ROUNDED_ON_VECTOR = (1856, 640, 0)
+LATE_PIECES = (128, 128, 256)
 
 
 def tile_picked_fpn_relu_e_kernel(
@@ -50,12 +49,8 @@ def tile_picked_fpn_relu_e_kernel(
             nc.sync.dma_start(codes[:], words[0].rearrange("p n t -> p (n t)").bitcast(I32))
             return codes
 
-        def quantize(grouped, planes, name):
-            codes = keep.tile([P, grouped.shape[1]], U32, name=name, align_bytes=64)
-            nc.vector.quantize_mx(
-                out=codes[:].bitcast(FP8X4), scales=planes[:], in_=grouped.rearrange("p c j -> p (c j)")
-            )
-            return codes
+        def quantize(grouped, codes, planes):
+            nc.vector.quantize_mx(out=codes.bitcast(FP8X4), scales=planes, in_=grouped.rearrange("p c j -> p (c j)"))
 
         def product(acc, w_codes, w_planes, block, codes, planes):
             cols = slice(block * P, (block + 1) * P)
@@ -90,12 +85,10 @@ def tile_picked_fpn_relu_e_kernel(
         nc.sync.dma_start(x_plane[1][:], x_rows[:, 1, :])
         piece_planes = [
             keep.tile([P, width], U8, name="piece_planes%d" % n, align_bytes=64)
-            for n, width in enumerate((PIECE, PIECE, HALF))
+            for n, width in enumerate((PIECE,) * 4)
         ]
         nc.sync.dma_start(x_plane[2][:], x_rows[:, 2, :])
-        edges = [sum(LAST_CHUNKS[:c]) for c in range(len(LAST_CHUNKS) + 1)]
-        for c in range(len(LAST_CHUNKS)):
-            nc.sync.dma_start(x_plane[3][:, edges[c] : edges[c + 1]], x_rows[:, 3, edges[c] : edges[c + 1]])
+        nc.sync.dma_start(x_plane[3][:], x_rows[:, 3, :])
         w1_codes = load_words(w1_words, "w1_codes")
         w1_planes = keep.tile([P, N], U8, align_bytes=64)
         nc.gpsimd.memset(w1_planes[:], 0)
@@ -129,41 +122,46 @@ def tile_picked_fpn_relu_e_kernel(
             for h in range(2):
                 nc.vector.tensor_copy(parents[h][:, block, :], t_window[:].indirect(par_list[:, halves[h]]))
 
-        picked = [keep.tile([P, HALF, PACK], BF16, name="picked%d" % h, align_bytes=64) for h in range(2)]
-        dense = keep.tile([P, 3, S], BF16, name="dense")
+        first_half = keep.tile([P, HALF, PACK], BF16, align_bytes=64)
+        late = [
+            keep.tile([P, width, PACK], BF16, name="late%d" % n, align_bytes=64) for n, width in enumerate(LATE_PIECES)
+        ]
+        edges = [sum(LATE_PIECES[:n]) for n in range(len(LATE_PIECES) + 1)]
+        late_cols = [slice(edges[n], edges[n + 1]) for n in range(len(LATE_PIECES))]
+        low = keep.tile([P, 2, S], BF16)
         for j in range(2):
-            nc.vector.tensor_copy(dense[:, j, :], x_plane[j][:].indirect(offs_list[:]))
-        nc.scalar.copy(*side_by_side(picked[0][:, :, :2], dense[:, :2, :HALF]))
-        for first in range(0, HALF, PIECE):
-            cols = slice(HALF + first, HALF + first + PIECE)
-            entries = slice(cols.start // 16, cols.stop // 16)
-            nc.vector.tensor_copy(dense[:, 2, cols], x_plane[2][:].indirect(offs_list[:, entries]))
-            nc.scalar.copy(*side_by_side(picked[1][:, first : first + PIECE, :3], dense[:, :, cols]))
-        nc.vector.tensor_copy(picked[0][:, :, 2], x_plane[2][:].indirect(offs_list[:, halves[0]]))
+            nc.vector.tensor_copy(low[:, j, :], x_plane[j][:].indirect(offs_list[:]))
+        nc.scalar.copy(*side_by_side(first_half[:, :, :2], low[:, :, :HALF]))
+        for n, cols in enumerate(late_cols):
+            nc.scalar.copy(*side_by_side(late[n][:, :, :2], low[:, :, HALF + cols.start : HALF + cols.stop]))
 
-        x3_rounded = keep.tile([P, T], BF16)
-        for c in range(len(LAST_CHUNKS)):
-            cut = edges[c] + ROUNDED_ON_VECTOR[c]
-            if cut > edges[c]:
-                nc.vector.tensor_copy(x3_rounded[:, edges[c] : cut], x_plane[3][:, edges[c] : cut])
-            nc.scalar.activation(x3_rounded[:, cut : edges[c + 1]], x_plane[3][:, cut : edges[c + 1]], COPY)
-        nc.vector.tensor_copy(picked[0][:, :, 3], x_plane[3][:].indirect(offs_list[:, halves[0]]))
-        nc.scalar.activation(picked[1][:, :, 3], x3_rounded[:].indirect(offs_list[:, halves[1]]), COPY)
+        high = [keep.tile([P, 2, width], BF16, name="high%d" % n) for n, width in enumerate(LATE_PIECES)]
+        for j in range(2):
+            for n, cols in enumerate(late_cols):
+                entries = slice((HALF + cols.start) // 16, (HALF + cols.stop) // 16)
+                nc.scalar.activation(high[n][:, j, :], x_plane[2 + j][:].indirect(offs_list[:, entries]), COPY)
+            nc.vector.tensor_copy(first_half[:, :, 2 + j], x_plane[2 + j][:].indirect(offs_list[:, halves[0]]))
+        nc.vector.tensor_copy(late[0][:, :, 2:], high[0][:].rearrange("p j c -> p c j"))
+        for n in range(1, len(LATE_PIECES)):
+            nc.scalar.copy(late[n][:, :, 2:], high[n][:].rearrange("p j c -> p c j"))
 
         accs = {}
+        piece_codes = [keep.tile([P, PIECE], U32, name="piece_codes%d" % n, align_bytes=64) for n in range(4)]
         for n in range(HALF // PIECE):
             cols = slice(n * PIECE, (n + 1) * PIECE)
-            codes = quantize(picked[0][:, cols, :], piece_planes[n], "piece_codes%d" % n)
+            quantize(first_half[:, cols, :], piece_codes[n][:], piece_planes[n][:])
             for block in range(BLOCKS):
                 acc = psum.tile([P, PIECE], F32, name="first_acc%d%d" % (n, block))
-                product(acc[:], w1_codes, w1_planes, block, codes[:], piece_planes[n][:])
+                product(acc[:], w1_codes, w1_planes, block, piece_codes[n][:], piece_planes[n][:])
                 accs[0, block, n] = acc[:]
-        codes = quantize(picked[1][:], piece_planes[2], "second_codes")
+        for n, cols in enumerate(late_cols):
+            piece = 2 + cols.start // PIECE
+            part = slice(cols.start % PIECE, cols.start % PIECE + LATE_PIECES[n])
+            quantize(late[n][:], piece_codes[piece][:, part], piece_planes[piece][:, part])
         for block in range(BLOCKS):
             for n in range(HALF // PIECE):
-                cols = slice(n * PIECE, (n + 1) * PIECE)
                 acc = psum.tile([P, HALF], F32, name="second_acc%d%d" % (block, n), tag="bank%d" % (2 * block + n))
-                product(acc[:, :PIECE], w1_codes, w1_planes, block, codes[:, cols], piece_planes[2][:, cols])
+                product(acc[:, :PIECE], w1_codes, w1_planes, block, piece_codes[2 + n][:], piece_planes[2 + n][:])
                 accs[1, block, n] = acc[:, :PIECE]
 
         def add_parents(h, block, n, total):

@@ -128,22 +128,16 @@ def tile_picked_fpn_relu_e_kernel(
         ]
         edges = [sum(LATE_PIECES[:n]) for n in range(len(LATE_PIECES) + 1)]
         late_cols = [slice(edges[n], edges[n + 1]) for n in range(len(LATE_PIECES))]
-        low = keep.tile([P, 2, S], BF16)
-        for j in range(2):
-            nc.vector.tensor_copy(low[:, j, :], x_plane[j][:].indirect(offs_list[:]))
-        nc.scalar.copy(*side_by_side(first_half[:, :, :2], low[:, :, :HALF]))
-        for n, cols in enumerate(late_cols):
-            nc.scalar.copy(*side_by_side(late[n][:, :, :2], low[:, :, HALF + cols.start : HALF + cols.stop]))
-
-        high = [keep.tile([P, 2, width], BF16, name="high%d" % n) for n, width in enumerate(LATE_PIECES)]
-        for j in range(2):
+        for j in range(PACK):
+            dense = []
             for n, cols in enumerate(late_cols):
                 entries = slice((HALF + cols.start) // 16, (HALF + cols.stop) // 16)
-                nc.scalar.activation(high[n][:, j, :], x_plane[2 + j][:].indirect(offs_list[:, entries]), COPY)
-            nc.vector.tensor_copy(first_half[:, :, 2 + j], x_plane[2 + j][:].indirect(offs_list[:, halves[0]]))
-        nc.vector.tensor_copy(late[0][:, :, 2:], high[0][:].rearrange("p j c -> p c j"))
-        for n in range(1, len(LATE_PIECES)):
-            nc.scalar.copy(late[n][:, :, 2:], high[n][:].rearrange("p j c -> p c j"))
+                dense.append(keep.tile([P, LATE_PIECES[n]], BF16, name="dense%d%d" % (j, n)))
+                nc.scalar.activation(dense[n][:], x_plane[j][:].indirect(offs_list[:, entries]), COPY)
+            nc.vector.tensor_copy(first_half[:, :, j], x_plane[j][:].indirect(offs_list[:, halves[0]]))
+            nc.vector.tensor_copy(late[0][:, :, j], dense[0][:])
+            for n in range(1, len(LATE_PIECES)):
+                nc.scalar.copy(late[n][:, :, j], dense[n][:])
 
         accs = {}
         piece_codes = [keep.tile([P, PIECE], U32, name="piece_codes%d" % n, align_bytes=64) for n in range(4)]

@@ -24,7 +24,7 @@ PIECE = 256
 SPARE = 32
 W2_ROW = 4
 S_ON_VECTOR = 352
-LATE_PIECES = (128, 128, 256)
+LATE_PIECES = (128, 256, 128)
 
 
 def tile_picked_fpn_relu_e_kernel(
@@ -83,10 +83,7 @@ def tile_picked_fpn_relu_e_kernel(
         offs_list = keep.tile([P, S // 16], U16)
         nc.sync.dma_start(offs_list[:], offs)
         nc.sync.dma_start(x_plane[1][:], x_rows[:, 1, :])
-        piece_planes = [
-            keep.tile([P, width], U8, name="piece_planes%d" % n, align_bytes=64)
-            for n, width in enumerate((PIECE,) * 4)
-        ]
+        half_planes = [keep.tile([P, HALF], U8, name="half_planes%d" % h, align_bytes=64) for h in range(2)]
         nc.sync.dma_start(x_plane[2][:], x_rows[:, 2, :])
         nc.sync.dma_start(x_plane[3][:], x_rows[:, 3, :])
         w1_codes = load_words(w1_words, "w1_codes")
@@ -128,34 +125,38 @@ def tile_picked_fpn_relu_e_kernel(
         ]
         edges = [sum(LATE_PIECES[:n]) for n in range(len(LATE_PIECES) + 1)]
         late_cols = [slice(edges[n], edges[n + 1]) for n in range(len(LATE_PIECES))]
+        def gather_late(j, n, dense):
+            first = HALF + edges[n]
+            entries = offs_list[:, first // 16 : (first + LATE_PIECES[n]) // 16]
+            nc.scalar.activation(dense, x_plane[j][:].indirect(entries), COPY)
+
+        rows = keep.tile([P, PACK, LATE_PIECES[0]], BF16)
         for j in range(PACK):
-            dense = []
-            for n, cols in enumerate(late_cols):
-                entries = slice((HALF + cols.start) // 16, (HALF + cols.stop) // 16)
-                dense.append(keep.tile([P, LATE_PIECES[n]], BF16, name="dense%d%d" % (j, n)))
-                nc.scalar.activation(dense[n][:], x_plane[j][:].indirect(offs_list[:, entries]), COPY)
+            dense = [keep.tile([P, LATE_PIECES[n]], BF16, name="dense%d%d" % (j, n)) for n in (1, 2)]
+            gather_late(j, 0, rows[:, j, :])
+            for n in (1, 2):
+                gather_late(j, n, dense[n - 1][:])
+            for n in (1, 2):
+                nc.scalar.copy(late[n][:, :, j], dense[n - 1][:])
             nc.vector.tensor_copy(first_half[:, :, j], x_plane[j][:].indirect(offs_list[:, halves[0]]))
-            nc.vector.tensor_copy(late[0][:, :, j], dense[0][:])
-            for n in range(1, len(LATE_PIECES)):
-                nc.scalar.copy(late[n][:, :, j], dense[n][:])
+        nc.vector.tensor_copy(*side_by_side(late[0][:], rows[:]))
 
         accs = {}
-        piece_codes = [keep.tile([P, PIECE], U32, name="piece_codes%d" % n, align_bytes=64) for n in range(4)]
+        half_codes = [keep.tile([P, HALF], U32, name="half_codes%d" % h, align_bytes=64) for h in range(2)]
         for n in range(HALF // PIECE):
             cols = slice(n * PIECE, (n + 1) * PIECE)
-            quantize(first_half[:, cols, :], piece_codes[n][:], piece_planes[n][:])
+            quantize(first_half[:, cols, :], half_codes[0][:, cols], half_planes[0][:, cols])
             for block in range(BLOCKS):
                 acc = psum.tile([P, PIECE], F32, name="first_acc%d%d" % (n, block))
-                product(acc[:], w1_codes, w1_planes, block, piece_codes[n][:], piece_planes[n][:])
+                product(acc[:], w1_codes, w1_planes, block, half_codes[0][:, cols], half_planes[0][:, cols])
                 accs[0, block, n] = acc[:]
         for n, cols in enumerate(late_cols):
-            piece = 2 + cols.start // PIECE
-            part = slice(cols.start % PIECE, cols.start % PIECE + LATE_PIECES[n])
-            quantize(late[n][:], piece_codes[piece][:, part], piece_planes[piece][:, part])
+            quantize(late[n][:], half_codes[1][:, cols], half_planes[1][:, cols])
         for block in range(BLOCKS):
             for n in range(HALF // PIECE):
+                cols = slice(n * PIECE, (n + 1) * PIECE)
                 acc = psum.tile([P, HALF], F32, name="second_acc%d%d" % (block, n), tag="bank%d" % (2 * block + n))
-                product(acc[:, :PIECE], w1_codes, w1_planes, block, piece_codes[2 + n][:], piece_planes[2 + n][:])
+                product(acc[:, :PIECE], w1_codes, w1_planes, block, half_codes[1][:, cols], half_planes[1][:, cols])
                 accs[1, block, n] = acc[:, :PIECE]
 
         def add_parents(h, block, n, total):

@@ -44,9 +44,11 @@ def tile_picked_fpn_relu_e_kernel(
                     scales[0, 4 * q : 4 * q + 4, :].bitcast(I32),
                 )
 
-        def load_words(words, name):
+        def load_words(words, name, cuts):
             codes = keep.tile([P, N], I32, name=name, align_bytes=64)
-            nc.sync.dma_start(codes[:], words[0].rearrange("p n t -> p (n t)").bitcast(I32))
+            source = words[0].rearrange("p n t -> p (n t)").bitcast(I32)
+            for first, last in zip(cuts, cuts[1:]):
+                nc.sync.dma_start(codes[:, first:last], source[:, first:last])
             return codes
 
         def quantize(grouped, codes, planes):
@@ -74,19 +76,20 @@ def tile_picked_fpn_relu_e_kernel(
         nc.sync.dma_start(s_raw[:], sT.rearrange("(p j) c -> p j c", j=PACK))
         s_planes = keep.tile([P, V], U8, align_bytes=64)
         load_scales(w2_scales, s_planes, W2_ROW)
-        w2_codes = load_words(w2_words, "w2_codes")
+        w2_codes = load_words(w2_words, "w2_codes", (0, N))
         par_list = keep.tile([P, S // 16], U16)
         nc.sync.dma_start(par_list[:], par)
 
-        x_plane = [keep.tile([P, T], F32, name="x_plane%d" % j) for j in range(PACK)]
-        nc.sync.dma_start(x_plane[0][:], x_rows[:, 0, :])
+        x_low = keep.tile([P, 2, T], F32)
+        nc.sync.dma_start(x_low[:], x_rows[:, :2, :])
         offs_list = keep.tile([P, S // 16], U16)
         nc.sync.dma_start(offs_list[:], offs)
-        nc.sync.dma_start(x_plane[1][:], x_rows[:, 1, :])
         half_planes = [keep.tile([P, HALF], U8, name="half_planes%d" % h, align_bytes=64) for h in range(2)]
-        nc.sync.dma_start(x_plane[2][:], x_rows[:, 2, :])
-        nc.sync.dma_start(x_plane[3][:], x_rows[:, 3, :])
-        w1_codes = load_words(w1_words, "w1_codes")
+        x_high = [keep.tile([P, T], F32, name="x_high%d" % u, tag="high%d" % u, align_bytes=64) for u in range(2)]
+        for u in range(2):
+            nc.sync.dma_start(x_high[u][:], x_rows[:, 2 + u, :])
+        x_plane = [x_low[:, 0, :], x_low[:, 1, :], x_high[0][:], x_high[1][:]]
+        w1_codes = load_words(w1_words, "w1_codes", (0, P, N))
         w1_planes = keep.tile([P, N], U8, align_bytes=64)
         nc.gpsimd.memset(w1_planes[:], 0)
         load_scales(w1_scales, w1_planes, 0)
@@ -128,21 +131,31 @@ def tile_picked_fpn_relu_e_kernel(
         def gather_late(j, n, dense):
             first = HALF + edges[n]
             entries = offs_list[:, first // 16 : (first + LATE_PIECES[n]) // 16]
-            nc.scalar.activation(dense, x_plane[j][:].indirect(entries), COPY)
+            nc.scalar.activation(dense, x_plane[j].indirect(entries), COPY)
 
         rows = keep.tile([P, PACK, LATE_PIECES[0]], BF16)
-        for j in range(PACK):
-            dense = [keep.tile([P, LATE_PIECES[n]], BF16, name="dense%d%d" % (j, n)) for n in (1, 2)]
+        low = keep.tile([P, 2, HALF], F32)
+        for j in range(2):
+            nc.scalar.activation(low[:, j, :], x_plane[j].indirect(offs_list[:, halves[1]]), COPY)
+            nc.vector.tensor_copy(first_half[:, :, j], x_plane[j].indirect(offs_list[:, halves[0]]))
+        nc.scalar.copy(rows[:, :2, :], low[:, :, late_cols[0]])
+        for n in (1, 2):
+            nc.scalar.copy(late[n][:, :, :2], low[:, :, late_cols[n]].rearrange("p j c -> p c j"))
+        for j in range(2, PACK):
+            dense = {n: keep.tile([P, LATE_PIECES[n]], BF16, name="dense%d%d" % (j, n)) for n in (1, 2)}
+            gather_late(j, 1, dense[1][:])
             gather_late(j, 0, rows[:, j, :])
+            gather_late(j, 2, dense[2][:])
             for n in (1, 2):
-                gather_late(j, n, dense[n - 1][:])
-            for n in (1, 2):
-                nc.scalar.copy(late[n][:, :, j], dense[n - 1][:])
-            nc.vector.tensor_copy(first_half[:, :, j], x_plane[j][:].indirect(offs_list[:, halves[0]]))
+                nc.scalar.copy(late[n][:, :, j], dense[n][:])
+            nc.vector.tensor_copy(first_half[:, :, j], x_plane[j].indirect(offs_list[:, halves[0]]))
         nc.vector.tensor_copy(*side_by_side(late[0][:], rows[:]))
 
         accs = {}
-        half_codes = [keep.tile([P, HALF], U32, name="half_codes%d" % h, align_bytes=64) for h in range(2)]
+        half_codes = [
+            keep.tile([P, HALF], U32, name="half_codes%d" % h, tag="high%d" % (1 - h), align_bytes=64)
+            for h in range(2)
+        ]
         for n in range(HALF // PIECE):
             cols = slice(n * PIECE, (n + 1) * PIECE)
             quantize(first_half[:, cols, :], half_codes[0][:, cols], half_planes[0][:, cols])

@@ -24,7 +24,8 @@ PIECE = 256
 SPARE = 32
 W2_ROW = 4
 S_ON_VECTOR = 352
-LATE_PIECES = (128, 256, 128)
+WIDE, SHORT, LAST = (512, 768), (768, 896), (896, 1024)
+LATE_ORDER = (2, 3)
 
 
 def tile_picked_fpn_relu_e_kernel(
@@ -35,7 +36,8 @@ def tile_picked_fpn_relu_e_kernel(
         keep = ctx.enter_context(tc.tile_pool(name="keep", bufs=1))
         psum = ctx.enter_context(tc.psum_pool(name="psum", bufs=1))
 
-        x_rows = xT.rearrange("(p j) c -> p j c", j=PACK)
+        def entries(offsets, first, last):
+            return offsets[:, first // 16 : last // 16]
 
         def load_scales(scales, planes, row):
             for q in range(4):
@@ -72,6 +74,8 @@ def tile_picked_fpn_relu_e_kernel(
                 rows.rearrange("p j (c i) -> p c j i", i=4),
             )
 
+        x_rows = xT.rearrange("(p j) c -> p j c", j=PACK)
+
         s_raw = keep.tile([P, PACK, V], F32)
         nc.sync.dma_start(s_raw[:], sT.rearrange("(p j) c -> p j c", j=PACK))
         s_planes = keep.tile([P, V], U8, align_bytes=64)
@@ -84,8 +88,7 @@ def tile_picked_fpn_relu_e_kernel(
         nc.sync.dma_start(x_low[:], x_rows[:, :2, :])
         offs_list = keep.tile([P, S // 16], U16)
         nc.sync.dma_start(offs_list[:], offs)
-        half_planes = [keep.tile([P, HALF], U8, name="half_planes%d" % h, align_bytes=64) for h in range(2)]
-        x_high = [keep.tile([P, T], F32, name="x_high%d" % u, tag="high%d" % u, align_bytes=64) for u in range(2)]
+        x_high = [keep.tile([P, T], F32, name="x_high%d" % u) for u in range(2)]
         for u in range(2):
             nc.sync.dma_start(x_high[u][:], x_rows[:, 2 + u, :])
         x_plane = [x_low[:, 0, :], x_low[:, 1, :], x_high[0][:], x_high[1][:]]
@@ -94,8 +97,6 @@ def tile_picked_fpn_relu_e_kernel(
         nc.gpsimd.memset(w1_planes[:], 0)
         load_scales(w1_scales, w1_planes, 0)
 
-        halves = [slice(h * HALF // 16, (h + 1) * HALF // 16) for h in range(2)]
-
         s_grouped = keep.tile([P, V, PACK], BF16, align_bytes=64)
         for cols in (slice(0, PIECE), slice(PIECE, S_ON_VECTOR)):
             nc.vector.tensor_copy(*side_by_side(s_grouped[:, cols, :], s_raw[:, :, cols]))
@@ -103,12 +104,8 @@ def tile_picked_fpn_relu_e_kernel(
         s_codes = keep.tile([P, V], U32, align_bytes=64)
         s_cols = [slice(0, PIECE), slice(PIECE, V)]
         for cols in s_cols:
-            nc.vector.quantize_mx(
-                out=s_codes[:, cols].bitcast(FP8X4),
-                scales=s_planes[:, cols],
-                in_=s_grouped[:, cols, :].rearrange("p c j -> p (c j)"),
-            )
-        parents = [keep.tile([P, BLOCKS, HALF], F32, name="parents%d" % h) for h in range(2)]
+            quantize(s_grouped[:, cols, :], s_codes[:, cols], s_planes[:, cols])
+        parents = keep.tile([P, BLOCKS, S], F32)
         for block in range(BLOCKS):
             t_window = keep.tile([P, V + SPARE], F32, name="t_window%d" % block)
             nc.gpsimd.memset(t_window[:, V:], 0.0)
@@ -120,83 +117,78 @@ def tile_picked_fpn_relu_e_kernel(
                 else:
                     nc.scalar.copy(t_window[:, cols], acc[:, :PIECE])
             for h in range(2):
-                nc.vector.tensor_copy(parents[h][:, block, :], t_window[:].indirect(par_list[:, halves[h]]))
+                nc.vector.tensor_copy(
+                    parents[:, block, h * HALF : (h + 1) * HALF],
+                    t_window[:].indirect(entries(par_list, h * HALF, (h + 1) * HALF)),
+                )
 
-        first_half = keep.tile([P, HALF, PACK], BF16, align_bytes=64)
-        late = [
-            keep.tile([P, width, PACK], BF16, name="late%d" % n, align_bytes=64) for n, width in enumerate(LATE_PIECES)
-        ]
-        edges = [sum(LATE_PIECES[:n]) for n in range(len(LATE_PIECES) + 1)]
-        late_cols = [slice(edges[n], edges[n + 1]) for n in range(len(LATE_PIECES))]
-        def gather_late(j, n, dense):
-            first = HALF + edges[n]
-            entries = offs_list[:, first // 16 : (first + LATE_PIECES[n]) // 16]
-            nc.scalar.activation(dense, x_plane[j].indirect(entries), COPY)
+        cells = keep.tile([P, S, PACK], BF16, align_bytes=64)
 
-        rows = keep.tile([P, PACK, LATE_PIECES[0]], BF16)
-        low = keep.tile([P, 2, HALF], F32)
+        def gather_in_place(j, first, last):
+            nc.vector.tensor_copy(cells[:, first:last, j], x_plane[j].indirect(entries(offs_list, first, last)))
+
+        low = keep.tile([P, 2, S - WIDE[1]], F32)
         for j in range(2):
-            nc.scalar.activation(low[:, j, :], x_plane[j].indirect(offs_list[:, halves[1]]), COPY)
-            nc.vector.tensor_copy(first_half[:, :, j], x_plane[j].indirect(offs_list[:, halves[0]]))
-        nc.scalar.copy(rows[:, :2, :], low[:, :, late_cols[0]])
-        for n in (1, 2):
-            nc.scalar.copy(late[n][:, :, :2], low[:, :, late_cols[n]].rearrange("p j c -> p c j"))
+            nc.scalar.activation(low[:, j, :], x_plane[j].indirect(entries(offs_list, WIDE[1], S)), COPY)
+            gather_in_place(j, 0, WIDE[1])
+        nc.scalar.copy(cells[:, WIDE[1] :, :2], low[:].rearrange("p j c -> p c j"))
         for j in range(2, PACK):
-            dense = {n: keep.tile([P, LATE_PIECES[n]], BF16, name="dense%d%d" % (j, n)) for n in (1, 2)}
-            gather_late(j, 1, dense[1][:])
-            gather_late(j, 0, rows[:, j, :])
-            gather_late(j, 2, dense[2][:])
-            for n in (1, 2):
-                nc.scalar.copy(late[n][:, :, j], dense[n][:])
-            nc.vector.tensor_copy(first_half[:, :, j], x_plane[j].indirect(offs_list[:, halves[0]]))
-        nc.vector.tensor_copy(*side_by_side(late[0][:], rows[:]))
+            dense = {
+                part: keep.tile([P, part[1] - part[0]], BF16, name="dense%d_%d" % (j, part[0]))
+                for part in (WIDE, SHORT, LAST)
+            }
+            for part in (WIDE, SHORT):
+                nc.scalar.activation(dense[part][:], x_plane[j].indirect(entries(offs_list, *part)), COPY)
+            gather_in_place(j, 0, HALF)
+            nc.vector.tensor_copy(dense[LAST][:], x_plane[j].indirect(entries(offs_list, *LAST)))
+            for part in (WIDE, SHORT, LAST):
+                nc.scalar.copy(cells[:, part[0] : part[1], j], dense[part][:])
+
+        x_codes = keep.tile([P, S], U32, align_bytes=64)
+        x_planes = keep.tile([P, S], U8, align_bytes=64)
+        for first, last in ((0, PIECE), (PIECE, HALF), WIDE, SHORT, LAST):
+            quantize(cells[:, first:last, :], x_codes[:, first:last], x_planes[:, first:last])
 
         accs = {}
-        half_codes = [
-            keep.tile([P, HALF], U32, name="half_codes%d" % h, tag="high%d" % (1 - h), align_bytes=64)
-            for h in range(2)
-        ]
-        for n in range(HALF // PIECE):
+        for n in range(2):
             cols = slice(n * PIECE, (n + 1) * PIECE)
-            quantize(first_half[:, cols, :], half_codes[0][:, cols], half_planes[0][:, cols])
             for block in range(BLOCKS):
                 acc = psum.tile([P, PIECE], F32, name="first_acc%d%d" % (n, block))
-                product(acc[:], w1_codes, w1_planes, block, half_codes[0][:, cols], half_planes[0][:, cols])
-                accs[0, block, n] = acc[:]
-        for n, cols in enumerate(late_cols):
-            quantize(late[n][:], half_codes[1][:, cols], half_planes[1][:, cols])
+                product(acc[:], w1_codes, w1_planes, block, x_codes[:, cols], x_planes[:, cols])
+                accs[block, n] = acc[:]
         for block in range(BLOCKS):
-            for n in range(HALF // PIECE):
+            for n in LATE_ORDER:
                 cols = slice(n * PIECE, (n + 1) * PIECE)
-                acc = psum.tile([P, HALF], F32, name="second_acc%d%d" % (block, n), tag="bank%d" % (2 * block + n))
-                product(acc[:, :PIECE], w1_codes, w1_planes, block, half_codes[1][:, cols], half_planes[1][:, cols])
-                accs[1, block, n] = acc[:, :PIECE]
+                acc = psum.tile([P, HALF], F32, name="second_acc%d%d" % (block, n), tag="bank%d" % (2 * block + n - 2))
+                product(acc[:, :PIECE], w1_codes, w1_planes, block, x_codes[:, cols], x_planes[:, cols])
+                accs[block, n] = acc[:, :PIECE]
 
-        def add_parents(h, block, n, total):
-            nc.vector.tensor_tensor(
-                total, accs[h, block, n], parents[h][:, block, n * PIECE : (n + 1) * PIECE], ADD
-            )
+        def add_parents(block, n, total):
+            nc.vector.tensor_tensor(total, accs[block, n], parents[:, block, n * PIECE : (n + 1) * PIECE], ADD)
 
-        for n in range(HALF // PIECE):
+        for n in range(2):
             for block in range(BLOCKS):
                 total = keep.tile([P, PIECE], F32, name="total%d%d" % (n, block))
-                add_parents(0, block, n, total[:])
+                add_parents(block, n, total[:])
                 result = keep.tile([P, PIECE], F32, name="result%d%d" % (n, block))
                 nc.scalar.activation(result[:], total[:], RELU)
                 nc.sync.dma_start(out[block * P : (block + 1) * P, n * PIECE : (n + 1) * PIECE], result[:])
         for block in range(BLOCKS):
             total = keep.tile([P, HALF], F32, name="second_total%d" % block)
             result = keep.tile([P, HALF], F32, name="second_result%d" % block)
-            pieces = [slice(n * PIECE, (n + 1) * PIECE) for n in range(HALF // PIECE)]
-            for n, cols in enumerate(pieces):
-                if (block, n) != (BLOCKS - 1, 1):
-                    add_parents(1, block, n, total[:, cols])
+            for n in LATE_ORDER:
+                cols = slice((n - 2) * PIECE, (n - 1) * PIECE)
+                if (block, n) != (BLOCKS - 1, LATE_ORDER[-1]):
+                    add_parents(block, n, total[:, cols])
                     nc.scalar.activation(result[:, cols], total[:, cols], RELU)
                     continue
-                ends = [slice(PIECE + g * P, PIECE + (g + 1) * P) for g in range(2)]
+                ends = [slice(cols.start + g * P, cols.start + (g + 1) * P) for g in range(2)]
                 for g, part in enumerate(ends):
                     nc.vector.tensor_tensor(
-                        total[:, part], accs[1, block, n][:, g * P : (g + 1) * P], parents[1][:, block, part], ADD
+                        total[:, part],
+                        accs[block, n][:, g * P : (g + 1) * P],
+                        parents[:, block, HALF + part.start : HALF + part.stop],
+                        ADD,
                     )
                 for part in ends:
                     nc.vector.tensor_scalar_max(result[:, part], total[:, part], 0.0)

@@ -25,7 +25,6 @@ SPARE = 32
 W2_ROW = 4
 S_ON_VECTOR = 352
 WIDE, SHORT, LAST = (512, 768), (768, 896), (896, 1024)
-LATE_ORDER = (2, 3)
 
 
 def tile_picked_fpn_relu_e_kernel(
@@ -92,7 +91,7 @@ def tile_picked_fpn_relu_e_kernel(
         for u in range(2):
             nc.sync.dma_start(x_high[u][:], x_rows[:, 2 + u, :])
         x_plane = [x_low[:, 0, :], x_low[:, 1, :], x_high[0][:], x_high[1][:]]
-        w1_codes = load_words(w1_words, "w1_codes", (0, P, N))
+        w1_codes = load_words(w1_words, "w1_codes", (0, N))
         w1_planes = keep.tile([P, N], U8, align_bytes=64)
         nc.gpsimd.memset(w1_planes[:], 0)
         load_scales(w1_scales, w1_planes, 0)
@@ -144,52 +143,54 @@ def tile_picked_fpn_relu_e_kernel(
             for part in (WIDE, SHORT, LAST):
                 nc.scalar.copy(cells[:, part[0] : part[1], j], dense[part][:])
 
-        x_codes = keep.tile([P, S], U32, align_bytes=64)
-        x_planes = keep.tile([P, S], U8, align_bytes=64)
-        for first, last in ((0, PIECE), (PIECE, HALF), WIDE, SHORT, LAST):
-            quantize(cells[:, first:last, :], x_codes[:, first:last], x_planes[:, first:last])
+        x_codes = keep.tile([P, S - P], U32, align_bytes=64)
+        x_planes = keep.tile([P, S - P], U8, align_bytes=64)
+        place = {0: P, PIECE: P + PIECE, WIDE[0]: P + HALF, SHORT[0]: 0, LAST[0]: P}
+
+        def quantize_cells(first, last):
+            cols = slice(place[first], place[first] + last - first)
+            quantize(cells[:, first:last, :], x_codes[:, cols], x_planes[:, cols])
 
         accs = {}
-        for n in range(2):
-            cols = slice(n * PIECE, (n + 1) * PIECE)
-            for block in range(BLOCKS):
-                acc = psum.tile([P, PIECE], F32, name="first_acc%d%d" % (n, block))
-                product(acc[:], w1_codes, w1_planes, block, x_codes[:, cols], x_planes[:, cols])
-                accs[block, n] = acc[:]
-        for block in range(BLOCKS):
-            for n in LATE_ORDER:
-                cols = slice(n * PIECE, (n + 1) * PIECE)
-                acc = psum.tile([P, HALF], F32, name="second_acc%d%d" % (block, n), tag="bank%d" % (2 * block + n - 2))
-                product(acc[:, :PIECE], w1_codes, w1_planes, block, x_codes[:, cols], x_planes[:, cols])
-                accs[block, n] = acc[:, :PIECE]
 
-        def add_parents(block, n, total):
-            nc.vector.tensor_tensor(total, accs[block, n], parents[:, block, n * PIECE : (n + 1) * PIECE], ADD)
+        def multiply(block, n, tag):
+            cols = slice(place[n * PIECE], place[n * PIECE] + PIECE)
+            acc = psum.tile([P, HALF], F32, name="y_acc%d%d" % (block, n), tag=tag)
+            product(acc[:, :PIECE], w1_codes, w1_planes, block, x_codes[:, cols], x_planes[:, cols])
+            accs[block, n] = acc[:, :PIECE]
 
-        for n in range(2):
+        def finish(block, n, result):
+            total = keep.tile([P, PIECE], F32, name="total%d%d" % (block, n))
+            nc.vector.tensor_tensor(total[:], accs[block, n], parents[:, block, n * PIECE : (n + 1) * PIECE], ADD)
+            nc.scalar.activation(result, total[:], RELU)
+
+        def finish_and_store(block, n):
+            result = keep.tile([P, PIECE], F32, name="result%d%d" % (block, n))
+            finish(block, n, result[:])
+            nc.sync.dma_start(out[block * P : (block + 1) * P, n * PIECE : (n + 1) * PIECE], result[:])
+
+        for part in ((0, PIECE), (PIECE, HALF), WIDE, SHORT):
+            quantize_cells(*part)
+        for n in range(3):
             for block in range(BLOCKS):
-                total = keep.tile([P, PIECE], F32, name="total%d%d" % (n, block))
-                add_parents(block, n, total[:])
-                result = keep.tile([P, PIECE], F32, name="result%d%d" % (n, block))
-                nc.scalar.activation(result[:], total[:], RELU)
-                nc.sync.dma_start(out[block * P : (block + 1) * P, n * PIECE : (n + 1) * PIECE], result[:])
+                multiply(block, n, "bank%d" % ((4 + 2 * n + block) % 8))
         for block in range(BLOCKS):
-            total = keep.tile([P, HALF], F32, name="second_total%d" % block)
-            result = keep.tile([P, HALF], F32, name="second_result%d" % block)
-            for n in LATE_ORDER:
-                cols = slice((n - 2) * PIECE, (n - 1) * PIECE)
-                if (block, n) != (BLOCKS - 1, LATE_ORDER[-1]):
-                    add_parents(block, n, total[:, cols])
-                    nc.scalar.activation(result[:, cols], total[:, cols], RELU)
-                    continue
-                ends = [slice(cols.start + g * P, cols.start + (g + 1) * P) for g in range(2)]
-                for g, part in enumerate(ends):
-                    nc.vector.tensor_tensor(
-                        total[:, part],
-                        accs[block, n][:, g * P : (g + 1) * P],
-                        parents[:, block, HALF + part.start : HALF + part.stop],
-                        ADD,
-                    )
-                for part in ends:
-                    nc.vector.tensor_scalar_max(result[:, part], total[:, part], 0.0)
-            nc.sync.dma_start(out[block * P : (block + 1) * P, HALF:], result[:])
+            finish_and_store(block, 0)
+        quantize_cells(*LAST)
+        for block in range(BLOCKS):
+            multiply(block, 3, "bank%d" % (2 + block))
+        for block in range(BLOCKS):
+            finish_and_store(block, 1)
+        for n in (2, 3):
+            finish_and_store(0, n)
+        result = keep.tile([P, HALF], F32)
+        finish(1, 2, result[:, :PIECE])
+        total = keep.tile([P, PIECE], F32)
+        ends = [slice(g * P, (g + 1) * P) for g in range(2)]
+        for part in ends:
+            nc.vector.tensor_tensor(
+                total[:, part], accs[1, 3][:, part], parents[:, 1, 3 * PIECE + part.start : 3 * PIECE + part.stop], ADD
+            )
+        for part in ends:
+            nc.vector.tensor_scalar_max(result[:, PIECE + part.start : PIECE + part.stop], total[:, part], 0.0)
+        nc.sync.dma_start(out[P:, HALF:], result[:])

@@ -25,6 +25,7 @@ SPARE = 32
 W2_ROW = 4
 S_ON_VECTOR = 352
 WIDE, SHORT, LAST = (512, 768), (768, 896), (896, 1024)
+EDGES = (0, 128, 384, 640, 896, 1024)
 
 
 def tile_picked_fpn_relu_e_kernel(
@@ -143,54 +144,54 @@ def tile_picked_fpn_relu_e_kernel(
             for part in (WIDE, SHORT, LAST):
                 nc.scalar.copy(cells[:, part[0] : part[1], j], dense[part][:])
 
-        x_codes = keep.tile([P, S - P], U32, align_bytes=64)
-        x_planes = keep.tile([P, S - P], U8, align_bytes=64)
-        place = {0: P, PIECE: P + PIECE, WIDE[0]: P + HALF, SHORT[0]: 0, LAST[0]: P}
+        x_codes = keep.tile([P, LAST[0]], U32, align_bytes=64)
+        x_planes = keep.tile([P, LAST[0]], U8, align_bytes=64)
+
+        def place(first, last):
+            return slice(first, last) if first < LAST[0] else slice(EDGES[1], EDGES[1] + last - first)
 
         def quantize_cells(first, last):
-            cols = slice(place[first], place[first] + last - first)
-            quantize(cells[:, first:last, :], x_codes[:, cols], x_planes[:, cols])
+            quantize(cells[:, first:last, :], x_codes[:, place(first, last)], x_planes[:, place(first, last)])
 
         accs = {}
 
-        def multiply(block, n, tag):
-            cols = slice(place[n * PIECE], place[n * PIECE] + PIECE)
-            acc = psum.tile([P, HALF], F32, name="y_acc%d%d" % (block, n), tag=tag)
-            product(acc[:, :PIECE], w1_codes, w1_planes, block, x_codes[:, cols], x_planes[:, cols])
-            accs[block, n] = acc[:, :PIECE]
+        def multiply(n, banks):
+            cols = place(EDGES[n], EDGES[n + 1])
+            for block in range(BLOCKS):
+                acc = psum.tile([P, HALF], F32, name="y_acc%d%d" % (block, n), tag="bank%d" % banks[block])
+                accs[block, n] = acc[:, : cols.stop - cols.start]
+                product(accs[block, n], w1_codes, w1_planes, block, x_codes[:, cols], x_planes[:, cols])
 
-        def finish(block, n, result):
-            total = keep.tile([P, PIECE], F32, name="total%d%d" % (block, n))
-            nc.vector.tensor_tensor(total[:], accs[block, n], parents[:, block, n * PIECE : (n + 1) * PIECE], ADD)
-            nc.scalar.activation(result, total[:], RELU)
+        def add_parents(block, n):
+            total = keep.tile([P, EDGES[n + 1] - EDGES[n]], F32, name="total%d%d" % (block, n))
+            nc.vector.tensor_tensor(total[:], accs[block, n], parents[:, block, EDGES[n] : EDGES[n + 1]], ADD)
+            return total
 
         def finish_and_store(block, n):
-            result = keep.tile([P, PIECE], F32, name="result%d%d" % (block, n))
-            finish(block, n, result[:])
-            nc.sync.dma_start(out[block * P : (block + 1) * P, n * PIECE : (n + 1) * PIECE], result[:])
+            total = add_parents(block, n)
+            result = keep.tile([P, EDGES[n + 1] - EDGES[n]], F32, name="result%d%d" % (block, n))
+            nc.scalar.activation(result[:], total[:], RELU)
+            nc.sync.dma_start(out[block * P : (block + 1) * P, EDGES[n] : EDGES[n + 1]], result[:])
 
-        for part in ((0, PIECE), (PIECE, HALF), WIDE, SHORT):
+        for part in ((0, EDGES[1]), (EDGES[1], EDGES[2]), (EDGES[2], HALF), WIDE, SHORT):
             quantize_cells(*part)
-        for n in range(3):
-            for block in range(BLOCKS):
-                multiply(block, n, "bank%d" % ((4 + 2 * n + block) % 8))
+        for n in range(4):
+            multiply(n, (2 * n, 2 * n + 1))
         for block in range(BLOCKS):
             finish_and_store(block, 0)
+        finish_and_store(0, 1)
         quantize_cells(*LAST)
+        multiply(4, (0, 1))
+        finish_and_store(1, 1)
         for block in range(BLOCKS):
-            multiply(block, 3, "bank%d" % (2 + block))
+            finish_and_store(block, 2)
         for block in range(BLOCKS):
-            finish_and_store(block, 1)
-        for n in (2, 3):
-            finish_and_store(0, n)
-        result = keep.tile([P, HALF], F32)
-        finish(1, 2, result[:, :PIECE])
-        total = keep.tile([P, PIECE], F32)
-        ends = [slice(g * P, (g + 1) * P) for g in range(2)]
-        for part in ends:
-            nc.vector.tensor_tensor(
-                total[:, part], accs[1, 3][:, part], parents[:, 1, 3 * PIECE + part.start : 3 * PIECE + part.stop], ADD
-            )
-        for part in ends:
-            nc.vector.tensor_scalar_max(result[:, PIECE + part.start : PIECE + part.stop], total[:, part], 0.0)
-        nc.sync.dma_start(out[P:, HALF:], result[:])
+            result = keep.tile([P, S - EDGES[3]], F32, name="last_result%d" % block)
+            for n in (3, 4):
+                total = add_parents(block, n)
+                part = result[:, EDGES[n] - EDGES[3] : EDGES[n + 1] - EDGES[3]]
+                if (block, n) == (BLOCKS - 1, 4):
+                    nc.vector.tensor_scalar_max(part, total[:], 0.0)
+                else:
+                    nc.scalar.activation(part, total[:], RELU)
+            nc.sync.dma_start(out[block * P : (block + 1) * P, EDGES[3] :], result[:])

@@ -148,7 +148,7 @@ def tile_picked_fpn_relu_e_kernel(
         x_planes = keep.tile([P, LAST[0]], U8, align_bytes=64)
 
         def place(first, last):
-            return slice(first, last) if first < LAST[0] else slice(EDGES[1], EDGES[1] + last - first)
+            return slice(first, last) if first < LAST[0] else slice(0, last - first)
 
         def quantize_cells(first, last):
             quantize(cells[:, first:last, :], x_codes[:, place(first, last)], x_planes[:, place(first, last)])
@@ -179,12 +179,11 @@ def tile_picked_fpn_relu_e_kernel(
             multiply(n, (2 * n, 2 * n + 1))
         for block in range(BLOCKS):
             finish_and_store(block, 0)
-        finish_and_store(0, 1)
         quantize_cells(*LAST)
         multiply(4, (0, 1))
-        finish_and_store(1, 1)
-        for block in range(BLOCKS):
-            finish_and_store(block, 2)
+        for n in (1, 2):
+            for block in range(BLOCKS):
+                finish_and_store(block, n)
         for block in range(BLOCKS):
             result = keep.tile([P, S - EDGES[3]], F32, name="last_result%d" % block)
             for n in (3, 4):

@@ -24,7 +24,9 @@ PIECE = 256
 SPARE = 32
 W2_ROW = 4
 S_ON_VECTOR = 352
-WIDE, SHORT, LAST = (512, 768), (768, 896), (896, 1024)
+STEPPED, LAST = (128, 640), (896, 1024)
+ON_SCALAR = ((0, 128), (640, 768), (768, 896))
+LOW_ON_VECTOR = 768
 EDGES = (0, 128, 384, 640, 896, 1024)
 
 
@@ -127,24 +129,31 @@ def tile_picked_fpn_relu_e_kernel(
         def gather_in_place(j, first, last):
             nc.vector.tensor_copy(cells[:, first:last, j], x_plane[j].indirect(entries(offs_list, first, last)))
 
-        low = keep.tile([P, 2, S - WIDE[1]], F32)
+        def gather_on_scalar(dense, j, part):
+            nc.scalar.activation(dense[:], x_plane[j].indirect(entries(offs_list, *part)), COPY)
+
+        def lay(dense, j, part):
+            nc.scalar.copy(cells[:, part[0] : part[1], j], dense[:])
+
+        low = keep.tile([P, 2, S - LOW_ON_VECTOR], F32)
         for j in range(2):
-            nc.scalar.activation(low[:, j, :], x_plane[j].indirect(entries(offs_list, WIDE[1], S)), COPY)
-            gather_in_place(j, 0, WIDE[1])
-        nc.scalar.copy(cells[:, WIDE[1] :, :2], low[:].rearrange("p j c -> p c j"))
+            nc.scalar.activation(low[:, j, :], x_plane[j].indirect(entries(offs_list, LOW_ON_VECTOR, S)), COPY)
+            gather_in_place(j, 0, LOW_ON_VECTOR)
+        nc.scalar.copy(cells[:, LOW_ON_VECTOR:, :2], low[:].rearrange("p j c -> p c j"))
+
         for j in range(2, PACK):
             dense = {
-                part: keep.tile([P, part[1] - part[0]], BF16, name="dense%d_%d" % (j, part[0]))
-                for part in (WIDE, SHORT, LAST)
+                part: keep.tile([P, P], BF16, name="dense%d_%d" % (j, part[0]), tag="dense%d_%d" % (j, part[0]), align_bytes=64)
+                for part in ON_SCALAR + (LAST,)
             }
-            for part in (WIDE, SHORT):
-                nc.scalar.activation(dense[part][:], x_plane[j].indirect(entries(offs_list, *part)), COPY)
-            gather_in_place(j, 0, HALF)
+            for part in ON_SCALAR:
+                gather_on_scalar(dense[part], j, part)
+            gather_in_place(j, *STEPPED)
             nc.vector.tensor_copy(dense[LAST][:], x_plane[j].indirect(entries(offs_list, *LAST)))
-            for part in (WIDE, SHORT, LAST):
-                nc.scalar.copy(cells[:, part[0] : part[1], j], dense[part][:])
+            for part in ON_SCALAR + (LAST,):
+                lay(dense[part], j, part)
 
-        x_codes = keep.tile([P, LAST[0]], U32, align_bytes=64)
+        x_codes = keep.tile([P, LAST[0]], U32, tag="dense3_0", align_bytes=64)
         x_planes = keep.tile([P, LAST[0]], U8, align_bytes=64)
 
         def place(first, last):
@@ -173,8 +182,8 @@ def tile_picked_fpn_relu_e_kernel(
             nc.scalar.activation(result[:], total[:], RELU)
             nc.sync.dma_start(out[block * P : (block + 1) * P, EDGES[n] : EDGES[n + 1]], result[:])
 
-        for part in ((0, EDGES[1]), (EDGES[1], EDGES[2]), (EDGES[2], HALF), WIDE, SHORT):
-            quantize_cells(*part)
+        for n in range(4):
+            quantize_cells(EDGES[n], EDGES[n + 1])
         for n in range(4):
             multiply(n, (2 * n, 2 * n + 1))
         for block in range(BLOCKS):

from contextlib import ExitStack

import concourse.mybir as mybir

K, T, S, V, N = 512, 4096, 1024, 512, 256
FLOPS = 2 * K * N * (S + V)

F32 = mybir.dt.float32
BF16 = mybir.dt.bfloat16
I32 = mybir.dt.int32
U32 = mybir.dt.uint32
U16 = mybir.dt.uint16
U8 = mybir.dt.uint8
FP8X4 = mybir.dt.float8_e4m3fn_x4
COPY = mybir.ActivationFunctionType.Copy
RELU = mybir.ActivationFunctionType.Relu
ADD = mybir.AluOpType.add

P = 128
PACK = 4
BLOCKS = N // P
HALF = S // 2
PIECE = 256
SPARE = 32
W2_ROW = 4
S_ON_VECTOR = 352
STEPPED, LAST = (128, 640), (896, 1024)
ON_SCALAR = ((0, 128), (640, 768), (768, 896))
LOW_ON_VECTOR = 768
EDGES = (0, 128, 384, 640, 896, 1024)


def tile_picked_fpn_relu_e_kernel(
    tc, xT, sT, w1_words, w1_scales, w2_words, w2_scales, offs, par, out
):
    nc = tc.nc
    with ExitStack() as ctx:
        keep = ctx.enter_context(tc.tile_pool(name="keep", bufs=1))
        psum = ctx.enter_context(tc.psum_pool(name="psum", bufs=1))

        def entries(offsets, first, last):
            return offsets[:, first // 16 : last // 16]

        def load_scales(scales, planes, row):
            for q in range(4):
                nc.sync.dma_start(
                    planes[32 * q + row : 32 * q + row + 4, :N].bitcast(I32),
                    scales[0, 4 * q : 4 * q + 4, :].bitcast(I32),
                )

        def load_words(words, name, cuts):
            codes = keep.tile([P, N], I32, name=name, align_bytes=64)
            source = words[0].rearrange("p n t -> p (n t)").bitcast(I32)
            for first, last in zip(cuts, cuts[1:]):
                nc.sync.dma_start(codes[:, first:last], source[:, first:last])
            return codes

        def quantize(grouped, codes, planes):
            nc.vector.quantize_mx(out=codes.bitcast(FP8X4), scales=planes, in_=grouped.rearrange("p c j -> p (c j)"))

        def product(acc, w_codes, w_planes, block, codes, planes):
            cols = slice(block * P, (block + 1) * P)
            nc.tensor.matmul_mx(
                out=acc,
                lhsT=w_codes[:, cols].bitcast(FP8X4),
                lhsT_scale=w_planes[:, cols],
                rhs=codes.bitcast(FP8X4),
                rhs_scale=planes,
                start=True,
                stop=True,
            )

        def side_by_side(grouped, rows):
            return (
                grouped.rearrange("p (c i) j -> p c j i", i=4),
                rows.rearrange("p j (c i) -> p c j i", i=4),
            )

        x_rows = xT.rearrange("(p j) c -> p j c", j=PACK)

        s_raw = keep.tile([P, PACK, V], F32)
        nc.sync.dma_start(s_raw[:], sT.rearrange("(p j) c -> p j c", j=PACK))
        s_planes = keep.tile([P, V], U8, align_bytes=64)
        load_scales(w2_scales, s_planes, W2_ROW)
        w2_codes = load_words(w2_words, "w2_codes", (0, N))
        par_list = keep.tile([P, S // 16], U16)
        nc.sync.dma_start(par_list[:], par)

        x_low = keep.tile([P, 2, T], F32)
        nc.sync.dma_start(x_low[:], x_rows[:, :2, :])
        offs_list = keep.tile([P, S // 16], U16)
        nc.sync.dma_start(offs_list[:], offs)
        x_high = [keep.tile([P, T], F32, name="x_high%d" % u) for u in range(2)]
        for u in range(2):
            nc.sync.dma_start(x_high[u][:], x_rows[:, 2 + u, :])
        x_plane = [x_low[:, 0, :], x_low[:, 1, :], x_high[0][:], x_high[1][:]]
        w1_codes = load_words(w1_words, "w1_codes", (0, N))
        w1_planes = keep.tile([P, N], U8, align_bytes=64)
        nc.gpsimd.memset(w1_planes[:], 0)
        load_scales(w1_scales, w1_planes, 0)

        s_grouped = keep.tile([P, V, PACK], BF16, align_bytes=64)
        for cols in (slice(0, PIECE), slice(PIECE, S_ON_VECTOR)):
            nc.vector.tensor_copy(*side_by_side(s_grouped[:, cols, :], s_raw[:, :, cols]))
        nc.scalar.copy(*side_by_side(s_grouped[:, S_ON_VECTOR:, :], s_raw[:, :, S_ON_VECTOR:]))
        s_codes = keep.tile([P, V], U32, align_bytes=64)
        s_cols = [slice(0, PIECE), slice(PIECE, V)]
        for cols in s_cols:
            quantize(s_grouped[:, cols, :], s_codes[:, cols], s_planes[:, cols])
        parents = keep.tile([P, BLOCKS, S], F32)
        for block in range(BLOCKS):
            t_window = keep.tile([P, V + SPARE], F32, name="t_window%d" % block)
            nc.gpsimd.memset(t_window[:, V:], 0.0)
            for n, cols in enumerate(s_cols):
                acc = psum.tile([P, HALF], F32, name="t_acc%d%d" % (block, n), tag="bank%d" % (2 * block + n))
                product(acc[:, :PIECE], w2_codes, s_planes[W2_ROW:], block, s_codes[:, cols], s_planes[:, cols])
                if block == 0 and n == 1:
                    nc.vector.tensor_copy(t_window[:, cols], acc[:, :PIECE])
                else:
                    nc.scalar.copy(t_window[:, cols], acc[:, :PIECE])
            for h in range(2):
                nc.vector.tensor_copy(
                    parents[:, block, h * HALF : (h + 1) * HALF],
                    t_window[:].indirect(entries(par_list, h * HALF, (h + 1) * HALF)),
                )

        cells = keep.tile([P, S, PACK], BF16, align_bytes=64)

        def gather_in_place(j, first, last):
            nc.vector.tensor_copy(cells[:, first:last, j], x_plane[j].indirect(entries(offs_list, first, last)))

        def gather_on_scalar(dense, j, part):
            nc.scalar.activation(dense[:], x_plane[j].indirect(entries(offs_list, *part)), COPY)

        def lay(dense, j, part):
            nc.scalar.copy(cells[:, part[0] : part[1], j], dense[:])

        low = keep.tile([P, 2, S - LOW_ON_VECTOR], F32)
        for j in range(2):
            nc.scalar.activation(low[:, j, :], x_plane[j].indirect(entries(offs_list, LOW_ON_VECTOR, S)), COPY)
            gather_in_place(j, 0, LOW_ON_VECTOR)
        nc.scalar.copy(cells[:, LOW_ON_VECTOR:, :2], low[:].rearrange("p j c -> p c j"))

        for j in range(2, PACK):
            dense = {
                part: keep.tile([P, P], BF16, name="dense%d_%d" % (j, part[0]), tag="dense%d_%d" % (j, part[0]), align_bytes=64)
                for part in ON_SCALAR + (LAST,)
            }
            for part in ON_SCALAR:
                gather_on_scalar(dense[part], j, part)
            gather_in_place(j, *STEPPED)
            nc.vector.tensor_copy(dense[LAST][:], x_plane[j].indirect(entries(offs_list, *LAST)))
            for part in ON_SCALAR + (LAST,):
                lay(dense[part], j, part)

        x_codes = keep.tile([P, LAST[0]], U32, tag="dense3_0", align_bytes=64)
        x_planes = keep.tile([P, LAST[0]], U8, align_bytes=64)

        def place(first, last):
            return slice(first, last) if first < LAST[0] else slice(0, last - first)

        def quantize_cells(first, last):
            quantize(cells[:, first:last, :], x_codes[:, place(first, last)], x_planes[:, place(first, last)])

        accs = {}

        def multiply(n, banks):
            cols = place(EDGES[n], EDGES[n + 1])
            for block in range(BLOCKS):
                acc = psum.tile([P, HALF], F32, name="y_acc%d%d" % (block, n), tag="bank%d" % banks[block])
                accs[block, n] = acc[:, : cols.stop - cols.start]
                product(accs[block, n], w1_codes, w1_planes, block, x_codes[:, cols], x_planes[:, cols])

        def add_parents(block, n):
            total = keep.tile([P, EDGES[n + 1] - EDGES[n]], F32, name="total%d%d" % (block, n))
            nc.vector.tensor_tensor(total[:], accs[block, n], parents[:, block, EDGES[n] : EDGES[n + 1]], ADD)
            return total

        def finish_and_store(block, n):
            total = add_parents(block, n)
            result = keep.tile([P, EDGES[n + 1] - EDGES[n]], F32, name="result%d%d" % (block, n))
            nc.scalar.activation(result[:], total[:], RELU)
            nc.sync.dma_start(out[block * P : (block + 1) * P, EDGES[n] : EDGES[n + 1]], result[:])

        for n in range(4):
            quantize_cells(EDGES[n], EDGES[n + 1])
        for n in range(4):
            multiply(n, (2 * n, 2 * n + 1))
        for block in range(BLOCKS):
            finish_and_store(block, 0)
        quantize_cells(*LAST)
        multiply(4, (0, 1))
        for n in (1, 2):
            for block in range(BLOCKS):
                finish_and_store(block, n)
        for block in range(BLOCKS):
            result = keep.tile([P, S - EDGES[3]], F32, name="last_result%d" % block)
            for n in (3, 4):
                total = add_parents(block, n)
                part = result[:, EDGES[n] - EDGES[3] : EDGES[n + 1] - EDGES[3]]
                if (block, n) == (BLOCKS - 1, 4):
                    nc.vector.tensor_scalar_max(part, total[:], 0.0)
                else:
                    nc.scalar.activation(part, total[:], RELU)
            nc.sync.dma_start(out[block * P : (block + 1) * P, EDGES[3] :], result[:])
